import numpy as np, ml_dtypes
CORES = [2,3,42,43,82,83,122,123]
N = 8
BF = ml_dtypes.bfloat16
C, S, M, B, LB, A, CL = 4, 4096, 8, 128, 7, 20, 255
def fold(p):
    p = np.asarray(p, np.int64)[..., None, None]; n = np.arange(M)[:, None]; b = np.arange(B)[None, :]
    return ((n * p + b * (p >> LB)) >> 8).reshape(p.shape[:-2] + (M * B,))
def bend(t, a):
    return t + ((a * (t >> 3) ** 2) >> 12)
def trials(rng, a, h):
    v = bend(np.arange(S, dtype=np.int64), a[..., None]); last = np.sum(np.maximum.accumulate(v, -1) < S, -1) - 1
    p = np.maximum(256 * (last + 1) * h // (64 * M), 256); room = last - fold(p)[..., -1]
    return p, rng.integers(0, room[..., None] + 1, (N, 8, N * C)), room
def given(x, p, a, de):
    return {"x": x.reshape(N, 16, C * S).astype(np.float32).astype(BF), "pa": np.stack([p, a], -1).astype(np.int32), "de": de.astype(np.int32)}
def setup_inputs(rng):
    a = rng.integers(-A, A + 1, (N, 8)); p, de, room = trials(rng, a, rng.integers(32, 58, (N, 8)))
    return given(rng.integers(0, 16, (N, 16, C, S)), p, a, de)
def setup_inputs_ends(rng):
    a = rng.permuted(np.tile(np.array([-A, -A, -1, 0, 0, 1, A, A]), (N, 1)), axis=1)
    h = rng.permuted(np.tile(np.array([0, 0, 20, 40, 40, 60, 64, 64]), (N, 1)), axis=1)
    p, de, room = trials(rng, a, h); far = rng.permuted(np.tile(np.arange(N * C) % 2, (N, 8, 1)), axis=2)
    return given(rng.integers(0, 16, (N, 16, C, S)), p, a, far * room[..., None])
def setup_inputs_brink(rng):
    a = rng.integers(-A, A + 1, (N, 8)); p, de, room = trials(rng, a, rng.integers(32, 58, (N, 8)))
    u = rng.integers(0, 8, (N, 16, C, S)); return given(8 + (u == 0) - 1 * (u == 1), p, a, de)
def setup_inputs_alike(rng):
    a = np.repeat(rng.integers(-A, A + 1, (N, 1)), 8, axis=1); p, de, room = trials(rng, a, np.repeat(rng.integers(16, 61, (N, 1)), 8, axis=1))
    q = rng.integers(0, N); de[q] = de[q, :1]; return given(rng.integers(0, 16, (N, 16, C, S)), p, a, de)
def setup_inputs_spread(rng):
    a = rng.integers(-A, A + 1, (N, 8)); p, de, room = trials(rng, a, rng.integers(1, 65, (N, 8)))
    v = rng.integers(0, 16, (N, 16, C, S)); m = rng.integers(0, 16, (N, 16, C, 1)); up = rng.permutation(np.arange(16) % 2).reshape(1, 16, 1, 1)
    v = np.where(up == 1, np.maximum(v, m), np.minimum(v, m)); k = rng.permutation(16)[:3]; v[:, k[:2]] = 15; v[:, k[2]] = 0
    return given(v, p, a, de)
def check_inputs(d):
    try:
        bad = []; x = np.asarray(d["x"]).astype(np.float32); pa = np.asarray(d["pa"]).astype(np.int64); de = np.asarray(d["de"]).astype(np.int64)
        if x.shape != (N, 16, C * S) or pa.shape != (N, 8, 2) or de.shape != (N, 8, N * C): return ["shapes"]
        if not (np.isfinite(x).all() and (x == np.floor(x)).all() and x.min() >= 0 and x.max() <= 15): bad.append("samples")
        if pa[..., 0].min() < 256: bad.append("periods")
        if np.abs(pa[..., 1]).max() > A: bad.append("accelerations")
        if de.min() < 0: bad.append("delays")
        t = fold(pa[..., 0])[:, :, None, :] + de[..., None]
        if t.min() < 0 or t.max() >= S: bad.append("times")
        s = bend(t, pa[..., 1][:, :, None, None])
        if s.min() < 0 or s.max() >= S: bad.append("places")
        return bad
    except Exception:
        return ["form"]
def reference(x, pa, de):
    v = x.astype(np.float32).astype(np.int64).reshape(N, 16, C, S); y = np.zeros((N, 8, 16, B), np.int64)
    for r in range(N):
        for g in range(8):
            fp = fold(pa[r, g, 0]); a = int(pa[r, g, 1]); tot = np.zeros((16, M * B), np.int64)
            for q in range(N):
                for c in range(C):
                    tot += v[q, :, c][:, bend(fp + int(de[r, g, C * q + c]), a)]
            y[r, g] = np.add.reduce(np.minimum(tot, CL).reshape(16, M, B), axis=1)
    return {"y": y.reshape(N, 128, B).astype(np.float32)}

@@ -1,0 +1,415 @@
+from concourse.bass import DstId, RemoteDMATransfer
+from concourse.mybir import AluOpType as Op, ActivationFunctionType as Act
+
+MAGIC = 12582912.0
+HALF = 2047.5 / 4096.0
+CH = 4096
+KAPPA = 1.6
+BLOCKS = ((0, 1), (2, 3))
+OWN_CHUNKS = (((0,), (-9, -9, -8.999, -8.998, -8.997, -8.996)), ((1,), (-8.9, -8.9, -8.899, -8.898, -8.897, -8.896)),
+              ((2, 3), (-8.8, -8.8, 0.6, 0.7, 1.1, 1.6)))
+FIRST_CHUNKS = (((0, 1), (2.3, 2.8, 3.5, 3.6, 3.7, 3.8)), ((2, 3), (2.31, 3.3, 4.1, 4.6, 5.1, 5.6)))
+LOOK = 7.0
+
+SCRATCH = {
+    "wo": ("sbuf", [128, CH], "bfloat16"), "ws": ("sbuf", [128, CH], "bfloat16"),
+    "raw": ("sbuf", [128, 4], "int32"), "pf": ("sbuf", [128, 4], "float32"), "cf": ("sbuf", [128, 1], "float32"),
+    "pin": ("sbuf", [128, 16], "float32"), "ones": ("sbuf", [128, 4], "float32"),
+    "ic": ("sbuf", [128, 32], "int32"), "cm": ("sbuf", [128, 32], "float32"),
+    "it": ("sbuf", [128, 32], "float32"), "it2": ("sbuf", [128, 32], "float32"),
+    "ie": ("sbuf", [128, 4], "int32"), "iee": ("sbuf", [128, 4], "int32"), "ie2": ("sbuf", [128, 4], "int32"),
+    "e": ("sbuf", [128, 4], "float32"), "e2": ("sbuf", [128, 4], "float32"),
+    "jf": ("sbuf", [128, 128], "int32"), "f": ("sbuf", [128, 128], "float32"), "rhs": ("sbuf", [128, 512], "float32"),
+    "isel": ("sbuf", [128, 32], "int32"), "sel1": ("sbuf", [128, 32], "bfloat16"), "sel2": ("sbuf", [128, 32], "bfloat16"),
+    "onesb": ("sbuf", [128, 128], "bfloat16"), "ident": ("sbuf", [128, 128], "bfloat16"),
+    "gall": ("sbuf", [128, 32768], "bfloat16"),
+    "acc": ("sbuf", [128, 512], "float32"), "tot": ("sbuf", [128, 512], "int32"),
+    "ta": ("sbuf", [128, 512], "int32"), "tb": ("sbuf", [128, 512], "int32"),
+    "ca": ("sbuf", [128, 512], "bfloat16"), "cb": ("sbuf", [128, 512], "bfloat16"),
+    "ysb": ("sbuf", [128, 128], "float32"),
+    "u0": ("psum", [128, 512], "float32"), "u1": ("psum", [128, 512], "float32"), "zc": ("psum", [128, 512], "float32"),
+    "b0": ("psum", [128, 512], "float32"), "b1": ("psum", [128, 512], "float32"), "b2": ("psum", [128, 512], "float32"),
+    "ap": ("psum", [128, 512], "float32"), "yp": ("psum", [128, 512], "float32"),
+}
+for _d in range(4):
+    for _n, _t in (("mm", "float32"), ("w", "float32"), ("s", "int32"), ("v", "float32"), ("off", "uint16")):
+        SCRATCH["%s%d" % (_n, _d)] = ("sbuf", [128, 512], _t)
+    SCRATCH["l%d" % _d] = ("sbuf", [128, 128], "float32")
+    SCRATCH["as%d" % _d] = ("sbuf", [128, 4], "float32")
+    if _d:
+        SCRATCH["snd%d" % _d] = ("sbuf", [128, 512], "uint16")
+        SCRATCH["rcv%d" % _d] = ("sbuf", [128, 512], "uint16")
+SEMAPHORES = ["V", "S", "P", "G", "par", "xl", "xs", "xr", "ps", "out", "sent"] + ["pr%d" % k for k in range(4)] \
+    + ["ar%d%d" % (d, b) for d in range(1, 4) for b in range(2)]
+
+
+def rank_program(g, core, T, topo):
+    me = T.rank_of(core)
+    if me is None:
+        return
+    cores = list(T.cores)
+    chips = []
+    for c in cores:
+        if topo.chip(c) not in chips:
+            chips.append(topo.chip(c))
+    on = [[c for c in cores if topo.chip(c) == ch] for ch in chips]
+    k = chips.index(topo.chip(core))
+    pos = on[k].index(core)
+    sib = [c for c in on[k] if c != core][0]
+    q0, q1 = me, T.rank_of(sib)
+    peer = [on[(k + d) % 4][pos] for d in range(4)]
+
+    V, S, P = g.vector, g.scalar, g.tensor
+    queue = {"V": V, "S": S, "P": P, "G": g, "Y": g.sync}
+    cnt = {"V": 0, "S": 0, "P": 0, "G": 0}
+    seen = {}
+
+    def em(E, ins):
+        ins.then_inc(T.sem[E], 1)
+        cnt[E] += 1
+        return (E, cnt[E])
+
+    def need(E, *toks):
+        best = {}
+        for tk in toks:
+            if tk is not None:
+                best[tk[0]] = max(best.get(tk[0], 0), tk[1])
+        for s in best:
+            if seen.get((E, s), 0) < best[s]:
+                queue[E].wait_ge(T.sem[s], best[s])
+                seen[(E, s)] = best[s]
+
+    def gcomp(fn, *a, **kw):
+        need("G", ("G", cnt["G"]))
+        return em("G", fn(*a, **kw))
+
+    r1 = em("V", V.memset(T.raw[:, :], 1))
+    need("Y", r1)
+    g.sync.dma_start(T.raw[0:64, 0:4], T.de[:, :]).then_inc(T.sem.par, 16)
+    g.sync.dma_start(T.raw[112:128, 0:1], T.pa[:, :]).then_inc(T.sem.par, 16)
+    need("S", r1)
+    S.dma_start(T.raw[64:80, 0:1], T.pa[:, :]).then_inc(T.sem.par, 16)
+    S.dma_start(T.raw[80:96, 0:1], T.pa[:, :]).then_inc(T.sem.par, 16)
+    for c in range(4):
+        for hh, q in ((0, g.sync), (1, S)):
+            q.dma_start(T.wo[32 * c + 16 * hh:32 * c + 16 * hh + 16, :], T.x[:, CH * c:CH * c + CH]).then_inc(T.sem.xl, 16)
+    o1 = em("V", V.memset(T.ones[:, :], 1.0))
+    ob = em("V", V.memset(T.onesb[:, :], 1.0))
+
+    gcomp(g.iota, T.ic[0:64, :], [[8, 2], [0, 16]], 0, 1)
+    a1 = gcomp(g.iota, T.ic[64:128, :], [[8, 2], [0, 16]], 0, 4)
+    gcomp(g.iota, T.ie[0:64, :], [[-16, 4]], 0, 1)
+    a2 = gcomp(g.iota, T.ie[64:128, :], [[-4, 4]], 0, 1)
+    a6 = gcomp(g.iota, T.jf[0:64, :], [[q0 - q1, 2], [0, 64]], -q0, 1)
+    gcomp(g.iota, T.f[64:96, :], [[0, 16], [16, 8]], 0, 0, allow_small_or_imprecise_dtypes=True)
+    a5 = gcomp(g.iota, T.f[96:128, :], [[0, 2], [1, 8], [0, 8]], 0, 0, allow_small_or_imprecise_dtypes=True)
+    gcomp(g.iota, T.it[64:96, :], [[0, 2], [1, 16]], 0, 0, allow_small_or_imprecise_dtypes=True)
+    a7 = gcomp(g.affine_select, T.it2[64:96, :], T.it[64:96, :], [[0, 32]], Op.is_ge, 1.0, 15, -1)
+    need("V", a1)
+    v1 = em("V", V.tensor_scalar(T.ic[:, :], T.ic[:, :], 8, None, Op.bitwise_and))
+    need("V", a2)
+    em("V", V.tensor_scalar(T.iee[0:64, :], T.ie[0:64, :], 48, None, Op.bitwise_and))
+    v3 = em("V", V.tensor_scalar(T.iee[64:128, :], T.ie[64:128, :], 13, None, Op.bitwise_and))
+    v4 = em("V", V.tensor_scalar(T.ie2[96:128, :], T.ie[96:128, :], -3, None, Op.bitwise_and))
+    need("V", v1)
+    c1 = em("V", V.tensor_scalar(T.cm[:, :], T.ic[:, :], 0, None, Op.is_equal))
+    need("V", v3)
+    e1 = em("V", V.tensor_scalar(T.e[:, :], T.iee[:, :], 0, 1.0 / 2048, Op.is_equal, Op.mult))
+    need("V", v4)
+    e2 = em("V", V.tensor_scalar(T.e2[96:128, :], T.ie2[96:128, :], 49, 1.0 / 4096, Op.is_equal, Op.mult))
+
+    V.wait_ge(T.sem.par, 64)
+    p1 = em("V", V.tensor_scalar(T.raw[64:96, 0:1], T.raw[64:96, 0:1], 7, None, Op.arith_shift_right))
+    em("V", V.tensor_copy(T.pf[0:64, :], T.raw[0:64, :]))
+    need("V", p1)
+    p2 = em("V", V.tensor_copy(T.cf[64:128, :], T.raw[64:128, 0:1]))
+    need("V", p2, o1)
+    p3 = em("V", V.tensor_scalar(T.pf[64:128, :], T.ones[64:128, :], T.cf[64:128, 0:1], None, Op.mult))
+    need("V", a5)
+    em("V", V.memset(T.f[64:80, :], 1.0))
+    em("V", V.memset(T.f[96:112, :], -1023.5))
+    f0 = em("V", V.tensor_scalar(T.jf[0:64, :], T.jf[0:64, :], 7, None, Op.bitwise_and))
+    need("V", f0)
+    f1 = em("V", V.tensor_scalar(T.f[0:64, :], T.jf[0:64, :], 0, 256.0, Op.is_equal, Op.mult))
+    need("V", a7, c1)
+    c2 = em("V", V.tensor_tensor(T.cm[64:96, :], T.cm[64:96, :], T.it2[64:96, :], Op.mult))
+    need("V", f1, e1)
+    for p in range(4):
+        rh = em("V", V.tensor_scalar(T.rhs[:, 128 * p:128 * p + 128], T.f[:, :], T.e[:, p:p + 1], None, Op.mult))
+    need("G", p3)
+    m = topo.mask(core, peer[1]) & topo.mask(core, peer[2]) & topo.mask(core, peer[3])
+    ne = bin(m).count("1")
+    ids, outs = [], []
+    for d in (1, 2, 3):
+        rid, pid, _se = topo.addr(peer[d])
+        ids.append(DstId(rid=rid, pnc=pid))
+        outs.append(T.pin[:, 4 * (4 - d):4 * (4 - d) + 4])
+    g.remote_dma_fused([RemoteDMATransfer(dst_ids=ids, dma_engine_mask=m, remote_sem=T.sem["pr%d" % k],
+                                          srcs=[T.pf[:, :]], dsts=outs)], local_sem=T.sem.ps)
+    a8 = gcomp(g.iota, T.isel[:, :], [[-1, 32]], 0, 1)
+    g.wait_ge(T.sem.xl, 128)
+    rid, pid, _se = topo.addr(sib)
+    g.remote_dma(T.ws[:, :], T.wo[:, :], T.sem.xr, T.sem.xs, pid, rid, topo.mask(core, sib))
+    nx = len(topo.engines(core, sib))
+    need("G", ob)
+    idt = gcomp(g.affine_select, T.ident[:, :], T.onesb[:, :], [[-1, 128]], Op.is_equal, 0.0, 0, 1)
+
+    units = [(0, p, 0) for p in range(4)] + [(1, p, 0) for p in range(4)] + [(1, p, 1) for p in range(4)]
+    for d in (2, 3):
+        units += [(d, p, w) for p in range(4) for w in (0, 1)]
+    units += [(0, p, 1) for p in range(4)]
+    at = {u: float(i) for i, u in enumerate(units)}
+    END = float(len(units))
+    items = []
+    tok = {}
+    gat = {u: [] for u in units}
+    uuse = ([], [])
+    chunkno, chunkof = {}, {}
+
+    def put(key, E, fn, cost=0.0):
+        items.append((key, len(items), E, fn, cost))
+
+    def span(ps):
+        return 128 * ps[0], 128 * ps[-1] + 128
+
+    def lbuild(d):
+        def fn():
+            if d:
+                V.wait_ge(T.sem["pr%d" % ((k + d) % 4)], ne)
+            need("V", c2, p3)
+            for c in range(4):
+                col = T.pin[:, 4 * d + c:4 * d + c + 1] if d else T.pf[:, c:c + 1]
+                tok["l", d] = em("V", V.tensor_scalar(T["l%d" % d][:, 32 * c:32 * c + 32], T.cm[:, :], col, None, Op.mult))
+        return fn
+
+    def chunk(d, ps, keys, first):
+        i = len(chunkno) % 2
+        chunkno[d, ps] = i
+        for p in ps:
+            chunkof[d, p] = ps
+        lo, hi = span(ps)
+        n = hi - lo
+        U, use = T["u%d" % i], uuse[i]
+        MM, W, SS, VV, OFF, AS = [T["%s%d" % (nm, d)] for nm in ("mm", "w", "s", "v", "off", "as")]
+
+        def times():
+            need("P", tok["l", d], rh, e2, tok.get(("as", d - 1)), *use)
+            L = T["l%d" % d]
+            tok["u", d, ps] = em("P", P.matmul(U[:, 0:n], L[:, :], T.rhs[:, lo:hi], True, True))
+            if first:
+                tok["ap", d] = em("P", P.matmul(T["ap"][:, 4 * d:4 * d + 4], L[96:128, :], T.e2[96:128, :], True, True))
+
+        def squares():
+            need("S", tok["u", d, ps])
+            a = em("S", S.activation(MM[:, lo:hi], U[:, 0:n], Act.Identity, bias=MAGIC))
+            tok["mm", d, ps] = a
+            use.append(a)
+            need("S", a)
+            tok["w", d, ps] = em("S", S.activation(W[:, lo:hi], MM[:, lo:hi], Act.Square, bias=-MAGIC))
+
+        def acols():
+            need("V", tok["ap", d])
+            tok["as", d] = em("V", V.tensor_copy(AS[:, :], T["ap"][:, 4 * d:4 * d + 4]))
+
+        def part0():
+            need("V", tok["mm", d, ps])
+            tok["s", d, ps] = em("V", V.tensor_scalar(SS[:, lo:hi], U[:, 0:n], 8.0, 3.5 - 2048, Op.mult, Op.add))
+            use.append(tok["s", d, ps])
+
+        def part1():
+            need("V", tok["w", d, ps], tok["as", d], tok.get("zcfree"))
+            for p in ps:
+                c = 128 * p
+                tok["z", d, ps] = em("V", V.tensor_scalar(T.zc[:, c:c + 128], W[:, c:c + 128], AS[:, p:p + 1], -HALF,
+                                                           Op.mult, Op.add))
+
+        def part2():
+            need("V", tok["z", d, ps], tok["s", d, ps])
+            tok["v", d, ps] = tok["zcfree"] = em("V", V.tensor_tensor(VV[:, lo:hi], SS[:, lo:hi], T.zc[:, lo:hi], Op.add))
+
+        def part3():
+            need("V", tok["v", d, ps])
+            tok["off", d, ps] = em("V", V.tensor_scalar(OFF[:, lo:hi], VV[:, lo:hi], MAGIC, MAGIC - 2048, Op.add, Op.subtract))
+
+        put(keys[0], "P", times)
+        put(keys[1], "S", squares, 2 * n)
+        if first:
+            put(keys[2] - 0.0005, "V", acols, 64)
+        for j, fn in enumerate((part0, part1, part2, part3)):
+            put(keys[2 + j], "V", fn, n)
+
+    def ucol(u):
+        return 1024 * units.index(u)
+
+    def gather(u, E, h0, h1):
+        d, p, w = u
+        need_x = ("xr", nx) if w else ("xl", 128)
+        if (need_x, E) not in tok:
+            tok[need_x, E] = 1
+            queue[E].wait_ge(T.sem[need_x[0]], need_x[1])
+        need(E, tok["off", d, chunkof[d, p]])
+        o = 128 * p + 64 * w
+        c = ucol(u)
+        ind = (T.ws if w else T.wo)[:, 0:CH].indirect(T["off%d" % d][:, o + 32 * h0:o + 32 * h1])
+        out = T.gall[:, c + 512 * h0:c + 512 * h1]
+        gat[u].append(em(E, V.tensor_copy(out, ind) if E == "V" else S.activation(out, ind, Act.Copy)))
+
+    buse = ([], [], [])
+    nb = [0]
+    sl = {}
+    nsent, nout = [0], [0]
+
+    def block(d, ps, j):
+        b = nb[0] % 3
+        nb[0] += 1
+        lo, hi = span(ps)
+        L = 32 * len(ps)
+        B = T["b%d" % b]
+
+        def sums(p):
+            def fn():
+                need("P", sl[0], *(gat[d, p, 0] + gat[d, p, 1] + buse[b]))
+                for n in range(4):
+                    c0 = L * n + 32 * (p - ps[0])
+                    for i, (w, nn) in enumerate(((0, n), (0, n + 4), (1, n), (1, n + 4))):
+                        c = ucol((d, p, w)) + 128 * nn
+                        ins = P.matmul(B[:, c0:c0 + 32], T.gall[:, c:c + 128], (T.sel2 if nn > 3 else T.sel1)[:, :], i == 0, i == 3)
+                tok["sum", d, p] = em("P", ins)
+            return fn
+
+        def evac():
+            need("V", *[tok["sum", d, p] for p in ps])
+            tok["ev", d, j] = em("V", V.tensor_copy(T["snd%d" % d][:, lo:hi], B[:, 0:hi - lo]))
+            buse[b].append(tok["ev", d, j])
+
+        def send():
+            need("G", tok["ev", d, j])
+            rid, pid, _se = topo.addr(peer[d])
+            g.remote_dma(T["rcv%d" % d][:, lo:hi], T["snd%d" % d][:, lo:hi], T.sem["ar%d%d" % (d, j)], T.sem.sent,
+                         pid, rid, topo.mask(core, peer[d]))
+            nsent[0] += len(topo.engines(core, peer[d]))
+
+        for p in ps:
+            put(at[d, p, 1] + 0.5, "P", sums(p))
+        if d:
+            key = min(at[d, ps[-1], 1] + (1.7 if d == 3 else 2.2), END + 0.05)
+            put(key, "V", evac, 128 * len(ps))
+            put(key, "G", send)
+        return b
+
+    def unpack(d, j, ps):
+        lo, hi = span(ps)
+
+        def fn():
+            V.wait_ge(T.sem["ar%d%d" % (d, j)], len(topo.engines(peer[4 - d], core)))
+            R = T["rcv%d" % d]
+            if ("acc", j) not in tok:
+                tok["acc", j] = em("V", V.tensor_copy(T.acc[:, lo:hi], R[:, lo:hi]))
+                return
+            X, free = (T.zc, "zcfree") if d == 3 else (T.yp, "ypfree")
+            need("V", tok.get(free))
+            a = em("V", V.tensor_copy(X[:, lo:hi], R[:, lo:hi]))
+            need("V", a, tok["acc", j])
+            tok[free] = tok["acc", j] = em("V", V.tensor_tensor(T.acc[:, lo:hi], T.acc[:, lo:hi], X[:, lo:hi], Op.add))
+        return fn
+
+    def finish(j, ps, b):
+        lo, hi = span(ps)
+
+        def fn():
+            need("V", tok["acc", j], *[tok["sum", 0, p] for p in ps])
+            t = em("V", V.tensor_tensor(T.tot[:, lo:hi], T.acc[:, lo:hi], T["b%d" % b][:, 0:hi - lo], Op.add))
+            need("V", t)
+            x1 = em("V", V.tensor_scalar(T.ta[:, lo:hi], T.tot[:, lo:hi], 511, None, Op.bitwise_and))
+            x2 = em("V", V.tensor_scalar(T.tb[:, lo:hi], T.tot[:, lo:hi], 9, None, Op.arith_shift_right))
+            need("V", x1)
+            tok["ca", j] = em("V", V.tensor_scalar(T.ca[:, lo:hi], T.ta[:, lo:hi], 255, None, Op.min))
+            need("V", x2)
+            tok["cb", j] = em("V", V.tensor_scalar(T.cb[:, lo:hi], T.tb[:, lo:hi], 255, None, Op.min))
+        return fn
+
+    def turn(j, ps):
+        L = 32 * len(ps)
+
+        def fn():
+            need("P", idt, tok["ca", j], tok["as", 3], tok["ypfree"])
+            O = T[("yp", "ap")[j]][32 * ps[0]:32 * ps[0] + L, 128 * j:128 * j + 128]
+            for i in range(8):
+                if i == 4:
+                    need("P", tok["cb", j])
+                c = 128 * ps[0] + L * (i % 4)
+                ins = P.matmul(O, (T.cb if i > 3 else T.ca)[:, c:c + L], T.ident[:, :], i == 0, i == 7)
+            tok["turn", j] = em("P", ins)
+        return fn
+
+    def leave(j, ps):
+        lo, hi = 32 * ps[0], 32 * ps[-1] + 32
+
+        def fn():
+            need("S", tok["turn", j])
+            t = em("S", S.activation(T.ysb[lo:hi, :], T[("yp", "ap")[j]][lo:hi, 128 * j:128 * j + 128], Act.Copy))
+            need("Y", t)
+            g.sync.dma_start(T.y[lo:hi, :], T.ysb[lo:hi, :]).then_inc(T.sem.out, 16)
+            nout[0] += 16
+        return fn
+
+    def selections():
+        need("V", a8)
+        x = em("V", V.tensor_scalar(T.isel[:, :], T.isel[:, :], 31, None, Op.bitwise_and))
+        need("V", x)
+        em("V", V.tensor_scalar(T.sel1[:, :], T.isel[:, :], 0, None, Op.is_equal))
+        sl[0] = em("V", V.tensor_scalar(T.sel2[:, :], T.isel[:, :], 0, 512.0, Op.is_equal, Op.mult))
+
+    put(27.0, "V", None, 1000.0)
+    put(-10, "V", lbuild(0), 256)
+    for i, (ps, keys) in enumerate(OWN_CHUNKS):
+        chunk(0, ps, keys, i == 0)
+    put(3.5, "V", selections, 200)
+    put(2.1, "V", lbuild(1), 256)
+    for i, (ps, keys) in enumerate(FIRST_CHUNKS):
+        chunk(1, ps, keys, i == 0)
+    for d in (2, 3):
+        put(at[d, 0, 0] - LOOK - 3.1, "V", lbuild(d), 256)
+        for i, ps in enumerate(BLOCKS):
+            x = at[d, ps[0], 0] - LOOK
+            chunk(d, ps, [x - 1.5, x, x + 1, x + 1.5, x + 2.0, x + 2.6], i == 0)
+    for d in (1, 2, 3):
+        for j, ps in enumerate(BLOCKS):
+            block(d, ps, j)
+            key = at[d, ps[-1], 1] + 9.2
+            if d == 3 or key > END + 0.1:
+                key = END + 0.1 + .1 * j
+            put(key, "V", unpack(d, j, ps), 256 * len(ps))
+    for j, ps in enumerate(BLOCKS):
+        b = block(0, ps, j)
+        put(END + 0.11 + .1 * j, "V", finish(j, ps, b))
+        put(END + 0.31 + .1 * j, "P", turn(j, ps))
+        put(END + 0.32 + .1 * j, "S", leave(j, ps))
+    for u in units:
+        put(at[u], "GATHER", u)
+
+    items.sort(key=lambda z: (z[0], z[1]))
+    load = {"V": 0.0, "S": 0.0}
+    for key, _i, E, fn, cost in items:
+        if E == "GATHER":
+            hs = []
+            for h in (0, 1):
+                e = "V" if load["V"] <= load["S"] else "S"
+                load[e] += 512 * KAPPA + 30
+                hs.append(e)
+            if hs[0] == hs[1]:
+                gather(fn, hs[0], 0, 2)
+            else:
+                gather(fn, hs[0], 0, 1)
+                gather(fn, hs[1], 1, 2)
+            continue
+        if E in load and key >= -0.3:
+            load[E] += cost
+        if fn is not None:
+            fn()
+    g.wait_ge(T.sem.out, nout[0])
+    g.wait_ge(T.sem.ps, ne)
+    g.wait_ge(T.sem.xs, nx)
+    g.wait_ge(T.sem.sent, nsent[0])
+    for E in ("V", "S", "P", "G"):
+        need("G", (E, cnt[E]))

@@ -5,42 +5,53 @@ MAGIC = 12582912.0
 HALF = 2047.5 / 4096.0
 CH = 4096
 KAPPA = 1.6
+FIRST = 3
+OWN_CHUNKS = (((0,), (-9, -9, -8.998, -8.997)), ((1,), (-8.9, -8.9, -8.898, -8.897)), ((2, 3), (-8.8, 0.2, 1.2, 1.6)))
+FIRST_CHUNKS = (((0, 1), (1.3, 1.8, 2.6, 2.7)), ((2, 3), (1.31, 2.3, 3.6, 4.1)))
+LATER_CHUNKS = (-8.2, -6.8, -5.9, -4.7)
 BLOCKS = ((0, 1), (2, 3))
-OWN_CHUNKS = (((0,), (-9, -9, -8.999, -8.998, -8.997, -8.996)), ((1,), (-8.9, -8.9, -8.899, -8.898, -8.897, -8.896)),
-              ((2, 3), (-8.8, -8.8, 0.6, 0.7, 1.1, 1.6)))
-FIRST_CHUNKS = (((0, 1), (2.3, 2.8, 3.5, 3.6, 3.7, 3.8)), ((2, 3), (2.31, 3.3, 4.1, 4.6, 5.1, 5.6)))
-LOOK = 7.0
+GROUPS = ((0, 1), (2,), (3,))
+EVAC, EVAC3 = 2.7, 1.6
+CREDIT = 3000.0
 
 SCRATCH = {
     "wo": ("sbuf", [128, CH], "bfloat16"), "ws": ("sbuf", [128, CH], "bfloat16"),
-    "raw": ("sbuf", [128, 4], "int32"), "pf": ("sbuf", [128, 4], "float32"), "cf": ("sbuf", [128, 1], "float32"),
-    "pin": ("sbuf", [128, 16], "float32"), "ones": ("sbuf", [128, 4], "float32"),
+    "raw": ("sbuf", [128, 4], "int32"), "pf": ("sbuf", [128, 4], "float32"), "ones": ("sbuf", [128, 4], "float32"),
+    "hq": ("sbuf", [128, 1], "int32"), "lr": ("sbuf", [128, 1], "int32"),
+    "a0": ("sbuf", [128, 1], "float32"), "a1": ("sbuf", [128, 1], "float32"),
+    "mi": ("sbuf", [128, 4], "int32"), "x17": ("sbuf", [128, 1], "int32"), "x48": ("sbuf", [128, 1], "int32"),
+    "x49": ("sbuf", [128, 1], "int32"), "m0": ("sbuf", [128, 1], "float32"), "m1": ("sbuf", [128, 1], "float32"),
+    "selr": ("sbuf", [128, 1], "float32"), "selq": ("sbuf", [128, 1], "float32"), "one1": ("sbuf", [128, 1], "float32"),
+    "sa": ("sbuf", [128, 1], "float32"), "sb": ("sbuf", [128, 1], "float32"), "sc": ("sbuf", [128, 1], "float32"),
     "ic": ("sbuf", [128, 32], "int32"), "cm": ("sbuf", [128, 32], "float32"),
-    "it": ("sbuf", [128, 32], "float32"), "it2": ("sbuf", [128, 32], "float32"),
+    "itr": ("sbuf", [128, 32], "float32"), "itk": ("sbuf", [128, 32], "float32"), "itm": ("sbuf", [128, 32], "float32"),
     "ie": ("sbuf", [128, 4], "int32"), "iee": ("sbuf", [128, 4], "int32"), "ie2": ("sbuf", [128, 4], "int32"),
-    "e": ("sbuf", [128, 4], "float32"), "e2": ("sbuf", [128, 4], "float32"),
-    "jf": ("sbuf", [128, 128], "int32"), "f": ("sbuf", [128, 128], "float32"), "rhs": ("sbuf", [128, 512], "float32"),
+    "io1": ("sbuf", [128, 4], "int32"), "oa": ("sbuf", [128, 4], "float32"), "ob": ("sbuf", [128, 4], "float32"),
+    "ea": ("sbuf", [128, 4], "float32"), "eb": ("sbuf", [128, 4], "float32"), "e2": ("sbuf", [128, 4], "float16"),
+    "jf": ("sbuf", [128, 128], "int32"), "f": ("sbuf", [128, 128], "float32"),
+    "fc": ("sbuf", [128, 64], "float32"), "fn": ("sbuf", [128, 64], "float32"),
+    "rha": ("sbuf", [128, 512], "float16"), "rhb": ("sbuf", [128, 512], "float16"),
+    "l0": ("sbuf", [128, 128], "float16"), "lin": ("sbuf", [128, 512], "float16"),
+    "mg": ("sbuf", [128, 512], "bfloat16"), "zer": ("sbuf", [128, 256], "bfloat16"),
     "isel": ("sbuf", [128, 32], "int32"), "sel1": ("sbuf", [128, 32], "bfloat16"), "sel2": ("sbuf", [128, 32], "bfloat16"),
-    "onesb": ("sbuf", [128, 128], "bfloat16"), "ident": ("sbuf", [128, 128], "bfloat16"),
+    "isel2": ("sbuf", [128, 16], "int32"), "selb": ("sbuf", [128, 16], "bfloat16"), "onesb": ("sbuf", [128, 128], "bfloat16"),
     "gall": ("sbuf", [128, 32768], "bfloat16"),
     "acc": ("sbuf", [128, 512], "float32"), "tot": ("sbuf", [128, 512], "int32"),
     "ta": ("sbuf", [128, 512], "int32"), "tb": ("sbuf", [128, 512], "int32"),
     "ca": ("sbuf", [128, 512], "bfloat16"), "cb": ("sbuf", [128, 512], "bfloat16"),
     "ysb": ("sbuf", [128, 128], "float32"),
-    "u0": ("psum", [128, 512], "float32"), "u1": ("psum", [128, 512], "float32"), "zc": ("psum", [128, 512], "float32"),
-    "b0": ("psum", [128, 512], "float32"), "b1": ("psum", [128, 512], "float32"), "b2": ("psum", [128, 512], "float32"),
-    "ap": ("psum", [128, 512], "float32"), "yp": ("psum", [128, 512], "float32"),
 }
+for _n in ("A0", "A1", "B0", "B1", "s0", "s1", "xb", "yp"):
+    SCRATCH[_n] = ("psum", [128, 512], "float32")
 for _d in range(4):
-    for _n, _t in (("mm", "float32"), ("w", "float32"), ("s", "int32"), ("v", "float32"), ("off", "uint16")):
+    for _n, _t in (("w", "float32"), ("z", "float32"), ("v", "float32"), ("off", "uint16")):
         SCRATCH["%s%d" % (_n, _d)] = ("sbuf", [128, 512], _t)
-    SCRATCH["l%d" % _d] = ("sbuf", [128, 128], "float32")
     SCRATCH["as%d" % _d] = ("sbuf", [128, 4], "float32")
     if _d:
         SCRATCH["snd%d" % _d] = ("sbuf", [128, 512], "uint16")
         SCRATCH["rcv%d" % _d] = ("sbuf", [128, 512], "uint16")
 SEMAPHORES = ["V", "S", "P", "G", "par", "xl", "xs", "xr", "ps", "out", "sent"] + ["pr%d" % k for k in range(4)] \
-    + ["ar%d%d" % (d, b) for d in range(1, 4) for b in range(2)]
+    + ["ar%d%d" % (d, b) for d in range(1, 4) for b in range(len(BLOCKS))]
 
 
 def rank_program(g, core, T, topo):
@@ -83,87 +94,130 @@ def rank_program(g, core, T, topo):
         need("G", ("G", cnt["G"]))
         return em("G", fn(*a, **kw))
 
-    r1 = em("V", V.memset(T.raw[:, :], 1))
-    need("Y", r1)
-    g.sync.dma_start(T.raw[0:64, 0:4], T.de[:, :]).then_inc(T.sem.par, 16)
-    g.sync.dma_start(T.raw[112:128, 0:1], T.pa[:, :]).then_inc(T.sem.par, 16)
-    need("S", r1)
-    S.dma_start(T.raw[64:80, 0:1], T.pa[:, :]).then_inc(T.sem.par, 16)
-    S.dma_start(T.raw[80:96, 0:1], T.pa[:, :]).then_inc(T.sem.par, 16)
+    def vs(needs, out, in0, s1, s2, op0, op1=None):
+        need("V", *needs)
+        if op1 is None:
+            return em("V", V.tensor_scalar(out, in0, s1, None, op0))
+        return em("V", V.tensor_scalar(out, in0, s1, s2, op0, op1))
+
+    def vt(needs, out, in0, in1, op):
+        need("V", *needs)
+        return em("V", V.tensor_tensor(out, in0, in1, op))
+
+    for lo, q in ((64, g.sync), (80, S), (96, g.sync), (112, S)):
+        q.dma_start(T.raw[lo:lo + 16, 0:1], T.pa[:, :]).then_inc(T.sem.par, 16)
+        if lo == 64:
+            q.dma_start(T.raw[0:64, 0:4], T.de[:, :]).then_inc(T.sem.par, 16)
     for c in range(4):
         for hh, q in ((0, g.sync), (1, S)):
             q.dma_start(T.wo[32 * c + 16 * hh:32 * c + 16 * hh + 16, :], T.x[:, CH * c:CH * c + CH]).then_inc(T.sem.xl, 16)
-    o1 = em("V", V.memset(T.ones[:, :], 1.0))
-    ob = em("V", V.memset(T.onesb[:, :], 1.0))
 
+    imp = {"allow_small_or_imprecise_dtypes": True}
+    i1 = gcomp(g.iota, T.mi[64:128, :], [[0, 4]], 0, 1)
+    gcomp(g.iota, T.itr[64:96, :], [[0, 8], [1, 4]], -1, 0, **imp)
+    i6 = gcomp(g.iota, T.itk[64:96, :], [[0, 2], [4, 4], [0, 4]], -8, 0, **imp)
     gcomp(g.iota, T.ic[0:64, :], [[8, 2], [0, 16]], 0, 1)
-    a1 = gcomp(g.iota, T.ic[64:128, :], [[8, 2], [0, 16]], 0, 4)
+    i7 = gcomp(g.iota, T.ic[64:128, :], [[8, 2], [0, 16]], 0, 4)
     gcomp(g.iota, T.ie[0:64, :], [[-16, 4]], 0, 1)
-    a2 = gcomp(g.iota, T.ie[64:128, :], [[-4, 4]], 0, 1)
-    a6 = gcomp(g.iota, T.jf[0:64, :], [[q0 - q1, 2], [0, 64]], -q0, 1)
-    gcomp(g.iota, T.f[64:96, :], [[0, 16], [16, 8]], 0, 0, allow_small_or_imprecise_dtypes=True)
-    a5 = gcomp(g.iota, T.f[96:128, :], [[0, 2], [1, 8], [0, 8]], 0, 0, allow_small_or_imprecise_dtypes=True)
-    gcomp(g.iota, T.it[64:96, :], [[0, 2], [1, 16]], 0, 0, allow_small_or_imprecise_dtypes=True)
-    a7 = gcomp(g.affine_select, T.it2[64:96, :], T.it[64:96, :], [[0, 32]], Op.is_ge, 1.0, 15, -1)
-    need("V", a1)
-    v1 = em("V", V.tensor_scalar(T.ic[:, :], T.ic[:, :], 8, None, Op.bitwise_and))
-    need("V", a2)
-    em("V", V.tensor_scalar(T.iee[0:64, :], T.ie[0:64, :], 48, None, Op.bitwise_and))
-    v3 = em("V", V.tensor_scalar(T.iee[64:128, :], T.ie[64:128, :], 13, None, Op.bitwise_and))
-    v4 = em("V", V.tensor_scalar(T.ie2[96:128, :], T.ie[96:128, :], -3, None, Op.bitwise_and))
-    need("V", v1)
-    c1 = em("V", V.tensor_scalar(T.cm[:, :], T.ic[:, :], 0, None, Op.is_equal))
-    need("V", v3)
-    e1 = em("V", V.tensor_scalar(T.e[:, :], T.iee[:, :], 0, 1.0 / 2048, Op.is_equal, Op.mult))
-    need("V", v4)
-    e2 = em("V", V.tensor_scalar(T.e2[96:128, :], T.ie2[96:128, :], 49, 1.0 / 4096, Op.is_equal, Op.mult))
+    i2 = gcomp(g.iota, T.ie[64:128, :], [[-4, 4]], 0, 1)
+    gcomp(g.iota, T.fc[96:128, :], [[16, 8], [128, 8]], 9, 0, **imp)
+    i4 = gcomp(g.iota, T.fn[96:128, :], [[0, 8], [1, 8]], 0, 0, **imp)
+    i5 = gcomp(g.iota, T.jf[0:64, :], [[q0 - q1, 2], [0, 64]], -q0, 1)
 
-    V.wait_ge(T.sem.par, 64)
-    p1 = em("V", V.tensor_scalar(T.raw[64:96, 0:1], T.raw[64:96, 0:1], 7, None, Op.arith_shift_right))
-    em("V", V.tensor_copy(T.pf[0:64, :], T.raw[0:64, :]))
-    need("V", p1)
-    p2 = em("V", V.tensor_copy(T.cf[64:128, :], T.raw[64:128, 0:1]))
-    need("V", p2, o1)
-    p3 = em("V", V.tensor_scalar(T.pf[64:128, :], T.ones[64:128, :], T.cf[64:128, 0:1], None, Op.mult))
-    need("V", a5)
-    em("V", V.memset(T.f[64:80, :], 1.0))
-    em("V", V.memset(T.f[96:112, :], -1023.5))
-    f0 = em("V", V.tensor_scalar(T.jf[0:64, :], T.jf[0:64, :], 7, None, Op.bitwise_and))
-    need("V", f0)
-    f1 = em("V", V.tensor_scalar(T.f[0:64, :], T.jf[0:64, :], 0, 256.0, Op.is_equal, Op.mult))
-    need("V", a7, c1)
-    c2 = em("V", V.tensor_tensor(T.cm[64:96, :], T.cm[64:96, :], T.it2[64:96, :], Op.mult))
-    need("V", f1, e1)
-    for p in range(4):
-        rh = em("V", V.tensor_scalar(T.rhs[:, 128 * p:128 * p + 128], T.f[:, :], T.e[:, p:p + 1], None, Op.mult))
-    need("G", p3)
-    m = topo.mask(core, peer[1]) & topo.mask(core, peer[2]) & topo.mask(core, peer[3])
-    ne = bin(m).count("1")
-    ids, outs = [], []
-    for d in (1, 2, 3):
-        rid, pid, _se = topo.addr(peer[d])
-        ids.append(DstId(rid=rid, pnc=pid))
-        outs.append(T.pin[:, 4 * (4 - d):4 * (4 - d) + 4])
-    g.remote_dma_fused([RemoteDMATransfer(dst_ids=ids, dma_engine_mask=m, remote_sem=T.sem["pr%d" % k],
-                                          srcs=[T.pf[:, :]], dsts=outs)], local_sem=T.sem.ps)
+    hi = slice(64, 128)
+    ands = Op.bitwise_and
+    o1 = em("V", V.memset(T.ones[:, :], 1.0))
+    vs([i1], T.x17[hi, :], T.mi[hi, 0:1], 17, None, ands)
+    vs([], T.x49[hi, :], T.mi[hi, 0:1], 49, None, ands)
+    xc = vs([], T.x48[hi, :], T.mi[hi, 0:1], 48, None, ands)
+    vs([xc], T.m0[hi, :], T.x17[hi, :], 0, None, Op.is_equal)
+    vs([], T.m1[hi, :], T.x17[hi, :], 16, None, Op.is_equal)
+    b3 = vs([], T.one1[hi, :], T.x49[hi, :], 1, None, Op.is_equal)
+    vs([], T.selr[hi, :], T.x48[hi, :], 48, None, Op.is_equal)
+    b4 = vs([], T.sa[hi, :], T.x49[hi, :], 49, 128.0, Op.is_equal, Op.mult)
+    need("S", b3, i6)
+    em("S", S.activation(T.itr[64:96, :], T.itr[64:96, :], Act.Copy, scale=T.m0[64:96, :]))
+    h1 = em("S", S.activation(T.itk[64:96, :], T.itk[64:96, :], Act.Identity, bias=T.one1[64:96, :], scale=T.m1[64:96, :]))
+    need("S", i4)
+    em("S", S.activation(T.fc[96:128, :], T.fc[96:128, :], Act.Copy, scale=T.m0[96:128, :]))
+    g2 = em("S", S.activation(T.fn[96:128, :], T.fn[96:128, :], Act.Copy, scale=T.m1[96:128, :]))
+    c1 = vs([b4], T.sb[hi, :], T.selr[hi, :], -1.0, T.sa[hi, :], Op.mult, Op.add)
+    h2 = vs([i7], T.ic[:, :], T.ic[:, :], 8, None, ands)
+    c3 = vs([c1], T.sc[hi, :], T.one1[hi, :], -1.0, T.sb[hi, :], Op.mult, Op.add)
+    h4 = vs([h2], T.cm[:, :], T.ic[:, :], 0, None, Op.is_equal)
+    h3 = vt([h1], T.itm[64:96, :], T.itr[64:96, :], T.itk[64:96, :], Op.add)
+    c4 = vs([c3], T.selq[hi, :], T.sc[hi, :], 1.0, None, Op.add)
+    h5 = vt([h3, h4], T.cm[64:96, :], T.cm[64:96, :], T.itm[64:96, :], Op.mult)
+    vs([i2], T.iee[0:64, :], T.ie[0:64, :], 48, None, ands)
+    vs([], T.iee[hi, :], T.ie[hi, :], 13, None, ands)
+    vs([], T.io1[64:96, :], T.ie[64:96, :], 61, None, ands)
+    xf = vs([], T.ie2[96:128, :], T.ie[96:128, :], -3, None, ands)
+
+    V.wait_ge(T.sem.par, 80)
+    vs([], T.hq[hi, :], T.raw[hi, 0:1], 7, None, Op.arith_shift_right)
+    p1 = vs([], T.lr[hi, :], T.raw[hi, 0:1], 127, None, ands)
+    vs([], T.pf[0:64, :], T.raw[0:64, :], 2048.0, None, Op.subtract)
+    p2 = vs([p1, c4], T.a0[hi, :], T.hq[hi, :], T.selq[hi, :], T.one1[hi, :], Op.mult, Op.add)
+    p3 = vs([p2], T.a1[hi, :], T.lr[hi, :], T.selr[hi, :], T.a0[hi, :], Op.mult, Op.add)
+    p4 = vs([p3, o1], T.pf[hi, :], T.ones[hi, :], T.a1[hi, :], None, Op.mult)
+    for c in range(4):
+        l0 = vs([p4, h5], T.l0[:, 32 * c:32 * c + 32], T.cm[:, :], T.pf[:, c:c + 1], None, Op.mult)
+    need("G", l0)
+    nps = [0]
+    came = {}
+    for ds in ((3,), (2, 1)):
+        m = topo.mask(core, peer[ds[0]]) & topo.mask(core, peer[ds[-1]])
+        ne = bin(m).count("1")
+        nps[0] += ne
+        ids, outs = [], []
+        for d in ds:
+            came[4 - d] = ne
+            rid, pid, _se = topo.addr(peer[d])
+            ids.append(DstId(rid=rid, pnc=pid))
+            outs.append(T.lin[:, 128 * (4 - d):128 * (4 - d) + 128])
+        g.remote_dma_fused([RemoteDMATransfer(dst_ids=ids, dma_engine_mask=m, remote_sem=T.sem["pr%d" % k],
+                                              srcs=[T.l0[:, :]], dsts=outs)], local_sem=T.sem.ps)
     a8 = gcomp(g.iota, T.isel[:, :], [[-1, 32]], 0, 1)
+
+    b5 = vs([xf], T.ea[:, :], T.iee[:, :], 0, 1.0 / 2048, Op.is_equal, Op.mult)
+    vs([], T.oa[64:96, :], T.io1[64:96, :], 1, -1023.5 / 2048, Op.is_equal, Op.mult)
+    vs([], T.ob[64:96, :], T.io1[64:96, :], 1, -127.5 / 256, Op.is_equal, Op.mult)
+    f0 = vs([i5], T.jf[0:64, :], T.jf[0:64, :], 7, None, ands)
+    c2 = vs([b5], T.eb[:, :], T.ea[:, :], 8.0, None, Op.mult)
+    vt([g2], T.f[96:128, 0:64], T.fc[96:128, :], T.fn[96:128, :], Op.add)
+    f2 = vt([], T.f[96:128, 64:128], T.fc[96:128, :], T.fn[96:128, :], Op.add)
+    vt([c2], T.ea[64:96, :], T.ea[64:96, :], T.oa[64:96, :], Op.add)
+    d2 = vt([], T.eb[64:96, :], T.eb[64:96, :], T.ob[64:96, :], Op.add)
+    em("V", V.memset(T.f[64:96, :], 1.0))
+    f1 = vs([f0], T.f[0:64, :], T.jf[0:64, :], 0, 256.0, Op.is_equal, Op.mult)
+    rh = {}
+
+    def right(p):
+        vs([f1, f2, d2], T.rha[:, 128 * p:128 * p + 128], T.f[:, :], T.ea[:, p:p + 1], None, Op.mult)
+        rh[p] = vs([], T.rhb[:, 128 * p:128 * p + 128], T.f[:, :], T.eb[:, p:p + 1], None, Op.mult)
+
+    em("V", V.memset(T.mg[0:1, :], MAGIC))
+    ob = em("V", V.memset(T.onesb[0:1, :], 1.0))
+    right(0)
+    e2 = vs([], T.e2[96:128, :], T.ie2[96:128, :], 49, 1.0 / 4096, Op.is_equal, Op.mult)
+
     g.wait_ge(T.sem.xl, 128)
     rid, pid, _se = topo.addr(sib)
     g.remote_dma(T.ws[:, :], T.wo[:, :], T.sem.xr, T.sem.xs, pid, rid, topo.mask(core, sib))
     nx = len(topo.engines(core, sib))
-    need("G", ob)
-    idt = gcomp(g.affine_select, T.ident[:, :], T.onesb[:, :], [[-1, 128]], Op.is_equal, 0.0, 0, 1)
 
-    units = [(0, p, 0) for p in range(4)] + [(1, p, 0) for p in range(4)] + [(1, p, 1) for p in range(4)]
+    units = [(0, p, 0) for p in range(FIRST)] + [(1, p, 0) for p in range(4)] + [(1, p, 1) for p in range(4)]
     for d in (2, 3):
         units += [(d, p, w) for p in range(4) for w in (0, 1)]
-    units += [(0, p, 1) for p in range(4)]
+    units += [(0, p, 0) for p in range(FIRST, 4)] + [(0, p, 1) for p in range(4)]
     at = {u: float(i) for i, u in enumerate(units)}
     END = float(len(units))
+    LAST = units[-1]
     items = []
     tok = {}
     gat = {u: [] for u in units}
-    uuse = ([], [])
+    use = {n: [] for n in ("A0", "A1", "B0", "B1", "s0", "s1", "xb", "yp")}
+    used = [0, 0]
     chunkno, chunkof = {}, {}
 
     def put(key, E, fn, cost=0.0):
@@ -172,16 +226,6 @@ def rank_program(g, core, T, topo):
     def span(ps):
         return 128 * ps[0], 128 * ps[-1] + 128
 
-    def lbuild(d):
-        def fn():
-            if d:
-                V.wait_ge(T.sem["pr%d" % ((k + d) % 4)], ne)
-            need("V", c2, p3)
-            for c in range(4):
-                col = T.pin[:, 4 * d + c:4 * d + c + 1] if d else T.pf[:, c:c + 1]
-                tok["l", d] = em("V", V.tensor_scalar(T["l%d" % d][:, 32 * c:32 * c + 32], T.cm[:, :], col, None, Op.mult))
-        return fn
-
     def chunk(d, ps, keys, first):
         i = len(chunkno) % 2
         chunkno[d, ps] = i
@@ -189,59 +233,55 @@ def rank_program(g, core, T, topo):
             chunkof[d, p] = ps
         lo, hi = span(ps)
         n = hi - lo
-        U, use = T["u%d" % i], uuse[i]
-        MM, W, SS, VV, OFF, AS = [T["%s%d" % (nm, d)] for nm in ("mm", "w", "s", "v", "off", "as")]
+        an, bn = "A%d" % i, "B%d" % i
+        A, B = T[an], T[bn]
+        W, Z, VV, OFF, AS = [T["%s%d" % (nm, d)] for nm in ("w", "z", "v", "off", "as")]
 
         def times():
-            need("P", tok["l", d], rh, e2, tok.get(("as", d - 1)), *use)
-            L = T["l%d" % d]
-            tok["u", d, ps] = em("P", P.matmul(U[:, 0:n], L[:, :], T.rhs[:, lo:hi], True, True))
-            if first:
-                tok["ap", d] = em("P", P.matmul(T["ap"][:, 4 * d:4 * d + 4], L[96:128, :], T.e2[96:128, :], True, True))
+            if d and first:
+                P.wait_ge(T.sem["pr%d" % ((k + d) % 4)], came[d])
+            assert len(use[an]) == len(use[bn]) == used[i]
+            used[i] += 1
+            need("P", l0, rh[ps[-1]], e2, ob, *(use[an] + use[bn]))
+            L = T.lin[:, 128 * d:128 * d + 128] if d else T.l0[:, :]
+            for bank, r in ((A, T.rha), (B, T.rhb)):
+                P.matmul(bank[:, 0:n], L, r[:, lo:hi], True, False)
+                tok[bank is A, d, ps] = em("P", P.matmul(bank[:, 0:n], T.onesb[0:1, :], T.mg[0:1, 0:n], False, True))
+                if first and bank is A:
+                    need("P", *use["yp"])
+                    L2 = T.lin[96:128, 128 * d:128 * d + 128] if d else T.l0[96:128, :]
+                    tok["ap", d] = em("P", P.matmul(T.yp[:, 4 * d:4 * d + 4], L2, T.e2[96:128, :], True, True))
 
         def squares():
-            need("S", tok["u", d, ps])
-            a = em("S", S.activation(MM[:, lo:hi], U[:, 0:n], Act.Identity, bias=MAGIC))
-            tok["mm", d, ps] = a
-            use.append(a)
-            need("S", a)
-            tok["w", d, ps] = em("S", S.activation(W[:, lo:hi], MM[:, lo:hi], Act.Square, bias=-MAGIC))
-
-        def acols():
-            need("V", tok["ap", d])
-            tok["as", d] = em("V", V.tensor_copy(AS[:, :], T["ap"][:, 4 * d:4 * d + 4]))
-
-        def part0():
-            need("V", tok["mm", d, ps])
-            tok["s", d, ps] = em("V", V.tensor_scalar(SS[:, lo:hi], U[:, 0:n], 8.0, 3.5 - 2048, Op.mult, Op.add))
-            use.append(tok["s", d, ps])
-
-        def part1():
-            need("V", tok["w", d, ps], tok["as", d], tok.get("zcfree"))
+            need("S", tok[True, d, ps])
+            a = em("S", S.activation(W[:, lo:hi], A[:, 0:n], Act.Square, bias=256.0 - MAGIC))
+            use[an].append(a)
+            if first:
+                need("S", tok["ap", d])
+                tok["as", d] = em("S", S.activation(AS[:, :], T.yp[:, 4 * d:4 * d + 4], Act.Copy))
+                use["yp"].append(tok["as", d])
+            need("S", a, tok["as", d])
             for p in ps:
                 c = 128 * p
-                tok["z", d, ps] = em("V", V.tensor_scalar(T.zc[:, c:c + 128], W[:, c:c + 128], AS[:, p:p + 1], -HALF,
-                                                           Op.mult, Op.add))
+                tok["z", d, ps] = em("S", S.activation(Z[:, c:c + 128], W[:, c:c + 128], Act.Identity, bias=-HALF, scale=AS[:, p:p + 1]))
 
-        def part2():
-            need("V", tok["z", d, ps], tok["s", d, ps])
-            tok["v", d, ps] = tok["zcfree"] = em("V", V.tensor_tensor(VV[:, lo:hi], SS[:, lo:hi], T.zc[:, lo:hi], Op.add))
+        def part0():
+            need("V", tok["z", d, ps], tok[False, d, ps])
+            tok["v", d, ps] = em("V", V.tensor_tensor(VV[:, lo:hi], B[:, 0:n], Z[:, lo:hi], Op.add))
+            use[bn].append(tok["v", d, ps])
 
-        def part3():
-            need("V", tok["v", d, ps])
-            tok["off", d, ps] = em("V", V.tensor_scalar(OFF[:, lo:hi], VV[:, lo:hi], MAGIC, MAGIC - 2048, Op.add, Op.subtract))
+        def part1():
+            tok["off", d, ps] = vs([tok["v", d, ps]], OFF[:, lo:hi], VV[:, lo:hi], MAGIC - 2048, None, Op.subtract)
 
         put(keys[0], "P", times)
-        put(keys[1], "S", squares, 2 * n)
-        if first:
-            put(keys[2] - 0.0005, "V", acols, 64)
-        for j, fn in enumerate((part0, part1, part2, part3)):
-            put(keys[2 + j], "V", fn, n)
+        put(keys[1], "S", squares, 2 * n + 64 * first)
+        put(keys[2], "V", part0, n)
+        put(keys[3], "V", part1, n)
 
     def ucol(u):
         return 1024 * units.index(u)
 
-    def gather(u, E, h0, h1):
+    def gather(u, E, z0, z1):
         d, p, w = u
         need_x = ("xr", nx) if w else ("xl", 128)
         if (need_x, E) not in tok:
@@ -250,37 +290,65 @@ def rank_program(g, core, T, topo):
         need(E, tok["off", d, chunkof[d, p]])
         o = 128 * p + 64 * w
         c = ucol(u)
-        ind = (T.ws if w else T.wo)[:, 0:CH].indirect(T["off%d" % d][:, o + 32 * h0:o + 32 * h1])
-        out = T.gall[:, c + 512 * h0:c + 512 * h1]
-        gat[u].append(em(E, V.tensor_copy(out, ind) if E == "V" else S.activation(out, ind, Act.Copy)))
+        ind = (T.ws if w else T.wo)[:, 0:CH].indirect(T["off%d" % d][:, o + 8 * z0:o + 8 * z1])
+        out = T.gall[:, c + 128 * z0:c + 128 * z1]
+        gat[u].append((z0, z1, em(E, V.tensor_copy(out, ind) if E == "V" else S.activation(out, ind, Act.Copy))))
 
-    buse = ([], [], [])
-    nb = [0]
     sl = {}
     nsent, nout = [0], [0]
+    nb = [0]
 
-    def block(d, ps, j):
-        b = nb[0] % 3
-        nb[0] += 1
-        lo, hi = span(ps)
-        L = 32 * len(ps)
-        B = T["b%d" % b]
+    def summing(bank, ps, d, lazy):
+        B = T[bank]
+        opened = []
 
-        def sums(p):
+        def one(u, z, start, stop):
+            c = ucol(u) + 128 * z
+            c0 = 128 * (u[1] - ps[0]) + 32 * (z % 4)
+            return P.matmul(B[:, c0:c0 + 32], T.gall[:, c:c + 128], (T.sel2 if z > 3 else T.sel1)[:, :], start, stop)
+
+        def whole(p):
             def fn():
-                need("P", sl[0], *(gat[d, p, 0] + gat[d, p, 1] + buse[b]))
-                for n in range(4):
-                    c0 = L * n + 32 * (p - ps[0])
-                    for i, (w, nn) in enumerate(((0, n), (0, n + 4), (1, n), (1, n + 4))):
-                        c = ucol((d, p, w)) + 128 * nn
-                        ins = P.matmul(B[:, c0:c0 + 32], T.gall[:, c:c + 128], (T.sel2 if nn > 3 else T.sel1)[:, :], i == 0, i == 3)
+                need("P", sl[0], *([t for w in (0, 1) for _a, _b, t in gat[d, p, w]] + use[bank]))
+                for z in range(4):
+                    for i, (w, zz) in enumerate(((0, z), (0, z + 4), (1, z), (1, z + 4))):
+                        ins = one((d, p, w), zz, i == 0, i == 3)
                 tok["sum", d, p] = em("P", ins)
             return fn
 
+        def part(p, w, last):
+            def fn():
+                if not opened:
+                    opened.append(1)
+                    n = 128 * len(ps)
+                    need("P", ob, tok["zer"], *use[bank])
+                    P.matmul(B[:, 0:n], T.onesb[0:1, :], T.zer[0:1, 0:n], True, False)
+                need("P", sl[0])
+                todo = sorted(gat[d, p, w], key=lambda q: (q[0] % 4, q[0]))
+                for i, (z0, z1, t) in enumerate(todo):
+                    need("P", t)
+                    for z in range(z0, z1):
+                        ins = one((d, p, w), z, False, last and i == len(todo) - 1 and z == z1 - 1)
+                tok["sum", d, p] = em("P", ins)
+            return fn
+
+        for p in ps:
+            if not lazy:
+                put(at[d, p, 1] + 0.5, "P", whole(p))
+            else:
+                for w in (0, 1):
+                    put(max(at[d, p, w] + (0.5 if d else 0.4), 21.5 + .01 * p), "P", part(p, w, w == 1 and p == ps[-1]))
+
+    def block(d, j, ps):
+        bank = "s%d" % (nb[0] % 2)
+        nb[0] += 1
+        lo, hi = span(ps)
+        summing(bank, ps, d, d == 3 and j == len(BLOCKS) - 1)
+
         def evac():
             need("V", *[tok["sum", d, p] for p in ps])
-            tok["ev", d, j] = em("V", V.tensor_copy(T["snd%d" % d][:, lo:hi], B[:, 0:hi - lo]))
-            buse[b].append(tok["ev", d, j])
+            tok["ev", d, j] = em("V", V.tensor_copy(T["snd%d" % d][:, lo:hi], T[bank][:, 0:hi - lo]))
+            use[bank].append(tok["ev", d, j])
 
         def send():
             need("G", tok["ev", d, j])
@@ -289,13 +357,9 @@ def rank_program(g, core, T, topo):
                          pid, rid, topo.mask(core, peer[d]))
             nsent[0] += len(topo.engines(core, peer[d]))
 
-        for p in ps:
-            put(at[d, p, 1] + 0.5, "P", sums(p))
-        if d:
-            key = min(at[d, ps[-1], 1] + (1.7 if d == 3 else 2.2), END + 0.05)
-            put(key, "V", evac, 128 * len(ps))
-            put(key, "G", send)
-        return b
+        key = at[d, ps[-1], 1] + (EVAC3 if d == 3 else EVAC)
+        put(key, "V", evac, 128 * len(ps))
+        put(key, "G", send)
 
     def unpack(d, j, ps):
         lo, hi = span(ps)
@@ -303,112 +367,118 @@ def rank_program(g, core, T, topo):
         def fn():
             V.wait_ge(T.sem["ar%d%d" % (d, j)], len(topo.engines(peer[4 - d], core)))
             R = T["rcv%d" % d]
-            if ("acc", j) not in tok:
-                tok["acc", j] = em("V", V.tensor_copy(T.acc[:, lo:hi], R[:, lo:hi]))
-                return
-            X, free = (T.zc, "zcfree") if d == 3 else (T.yp, "ypfree")
-            need("V", tok.get(free))
-            a = em("V", V.tensor_copy(X[:, lo:hi], R[:, lo:hi]))
-            need("V", a, tok["acc", j])
-            tok[free] = tok["acc", j] = em("V", V.tensor_tensor(T.acc[:, lo:hi], T.acc[:, lo:hi], X[:, lo:hi], Op.add))
+            if d == 1:
+                t = em("V", V.tensor_copy(T.acc[:, lo:hi], R[:, lo:hi]))
+            else:
+                need("V", *use["xb"])
+                a = em("V", V.tensor_copy(T.xb[:, lo:hi], R[:, lo:hi]))
+                need("V", a, *[tok["acc", p] for p in ps])
+                t = em("V", V.tensor_tensor(T.acc[:, lo:hi], T.acc[:, lo:hi], T.xb[:, lo:hi], Op.add))
+                use["xb"].append(t)
+            for p in ps:
+                tok["acc", p] = t
         return fn
 
-    def finish(j, ps, b):
+    def finish(j, ps, bank):
         lo, hi = span(ps)
 
         def fn():
-            need("V", tok["acc", j], *[tok["sum", 0, p] for p in ps])
-            t = em("V", V.tensor_tensor(T.tot[:, lo:hi], T.acc[:, lo:hi], T["b%d" % b][:, 0:hi - lo], Op.add))
-            need("V", t)
-            x1 = em("V", V.tensor_scalar(T.ta[:, lo:hi], T.tot[:, lo:hi], 511, None, Op.bitwise_and))
-            x2 = em("V", V.tensor_scalar(T.tb[:, lo:hi], T.tot[:, lo:hi], 9, None, Op.arith_shift_right))
-            need("V", x1)
-            tok["ca", j] = em("V", V.tensor_scalar(T.ca[:, lo:hi], T.ta[:, lo:hi], 255, None, Op.min))
-            need("V", x2)
-            tok["cb", j] = em("V", V.tensor_scalar(T.cb[:, lo:hi], T.tb[:, lo:hi], 255, None, Op.min))
+            t = vt([tok["acc", p] for p in ps] + [tok["sum", 0, p] for p in ps],
+                   T.tot[:, lo:hi], T.acc[:, lo:hi], T[bank][:, 0:hi - lo], Op.add)
+            use[bank].append(t)
+            x1 = vs([t], T.ta[:, lo:hi], T.tot[:, lo:hi], 511, None, Op.bitwise_and)
+            x2 = vs([], T.tb[:, lo:hi], T.tot[:, lo:hi], 9, None, Op.arith_shift_right)
+            tok["ca", j] = vs([x1], T.ca[:, lo:hi], T.ta[:, lo:hi], 255, None, Op.min)
+            tok["cb", j] = vs([x2], T.cb[:, lo:hi], T.tb[:, lo:hi], 255, None, Op.min)
         return fn
 
-    def turn(j, ps):
-        L = 32 * len(ps)
-
+    def turn(j, ps, bank):
         def fn():
-            need("P", idt, tok["ca", j], tok["as", 3], tok["ypfree"])
-            O = T[("yp", "ap")[j]][32 * ps[0]:32 * ps[0] + L, 128 * j:128 * j + 128]
-            for i in range(8):
-                if i == 4:
+            need("P", sl[0], tok["ca", j], *use[bank])
+            for z in range(8):
+                if z == 4:
                     need("P", tok["cb", j])
-                c = 128 * ps[0] + L * (i % 4)
-                ins = P.matmul(O, (T.cb if i > 3 else T.ca)[:, c:c + L], T.ident[:, :], i == 0, i == 7)
+                for p in ps:
+                    c = 128 * p + 32 * (z % 4)
+                    ins = P.matmul(T[bank][32 * p:32 * p + 32, 16 * z:16 * z + 16], (T.cb if z > 3 else T.ca)[:, c:c + 32],
+                                   T.selb[:, :], True, True)
             tok["turn", j] = em("P", ins)
         return fn
 
-    def leave(j, ps):
+    def leave(j, ps, bank):
         lo, hi = 32 * ps[0], 32 * ps[-1] + 32
 
         def fn():
             need("S", tok["turn", j])
-            t = em("S", S.activation(T.ysb[lo:hi, :], T[("yp", "ap")[j]][lo:hi, 128 * j:128 * j + 128], Act.Copy))
+            t = em("S", S.activation(T.ysb[lo:hi, :], T[bank][lo:hi, 0:128], Act.Copy))
             need("Y", t)
             g.sync.dma_start(T.y[lo:hi, :], T.ysb[lo:hi, :]).then_inc(T.sem.out, 16)
             nout[0] += 16
         return fn
 
-    def selections():
-        need("V", a8)
-        x = em("V", V.tensor_scalar(T.isel[:, :], T.isel[:, :], 31, None, Op.bitwise_and))
-        need("V", x)
-        em("V", V.tensor_scalar(T.sel1[:, :], T.isel[:, :], 0, None, Op.is_equal))
-        sl[0] = em("V", V.tensor_scalar(T.sel2[:, :], T.isel[:, :], 0, 512.0, Op.is_equal, Op.mult))
+    def later():
+        right(2)
+        right(3)
+        tok["zer"] = em("V", V.memset(T.zer[0:1, :], 0.0))
 
-    put(27.0, "V", None, 1000.0)
-    put(-10, "V", lbuild(0), 256)
+    def selections():
+        x = vs([a8], T.isel[:, :], T.isel[:, :], 31, None, Op.bitwise_and)
+        y = vs([x], T.isel2[:, :], T.isel[:, 0:16], 15, None, Op.bitwise_and)
+        vs([y], T.selb[:, :], T.isel2[:, :], 0, None, Op.is_equal)
+        vs([], T.sel1[:, :], T.isel[:, :], 0, None, Op.is_equal)
+        sl[0] = vs([], T.sel2[:, :], T.isel[:, :], 0, 512.0, Op.is_equal, Op.mult)
+
+    put(-9.5, "V", lambda: right(1))
+    put(-8.85, "V", later)
     for i, (ps, keys) in enumerate(OWN_CHUNKS):
         chunk(0, ps, keys, i == 0)
-    put(3.5, "V", selections, 200)
-    put(2.1, "V", lbuild(1), 256)
+    put(3.5, "V", selections, 320)
     for i, (ps, keys) in enumerate(FIRST_CHUNKS):
         chunk(1, ps, keys, i == 0)
     for d in (2, 3):
-        put(at[d, 0, 0] - LOOK - 3.1, "V", lbuild(d), 256)
         for i, ps in enumerate(BLOCKS):
-            x = at[d, ps[0], 0] - LOOK
-            chunk(d, ps, [x - 1.5, x, x + 1, x + 1.5, x + 2.0, x + 2.6], i == 0)
+            chunk(d, ps, [at[d, ps[0], 0] + c for c in LATER_CHUNKS], i == 0)
     for d in (1, 2, 3):
         for j, ps in enumerate(BLOCKS):
-            block(d, ps, j)
-            key = at[d, ps[-1], 1] + 9.2
-            if d == 3 or key > END + 0.1:
-                key = END + 0.1 + .1 * j
+            block(d, j, ps)
+            key = END + 0.01 + 0.09 * j if d == 3 else min(at[d, ps[-1], 1] + 9.2, END - 0.09)
             put(key, "V", unpack(d, j, ps), 256 * len(ps))
-    for j, ps in enumerate(BLOCKS):
-        b = block(0, ps, j)
-        put(END + 0.11 + .1 * j, "V", finish(j, ps, b))
-        put(END + 0.31 + .1 * j, "P", turn(j, ps))
-        put(END + 0.32 + .1 * j, "S", leave(j, ps))
+    for j, ps in enumerate(GROUPS):
+        bank, out = ("A0", "A1", "B0")[j], ("yp", "B1", "s0")[j]
+        summing(bank, ps, 0, True)
+        key = END + 0.05 * (1, 3, 4)[j]
+        put(key, "V", finish(j, ps, bank))
+        put(key + 0.02, "P", turn(j, ps, out))
+        put(key + 0.9, "S", leave(j, ps, out))
+    put(END - 5.01, "V", None, CREDIT)
     for u in units:
         put(at[u], "GATHER", u)
 
-    items.sort(key=lambda z: (z[0], z[1]))
+    items.sort(key=lambda it: (it[0], it[1]))
     load = {"V": 0.0, "S": 0.0}
     for key, _i, E, fn, cost in items:
         if E == "GATHER":
             hs = []
             for h in (0, 1):
                 e = "V" if load["V"] <= load["S"] else "S"
-                load[e] += 512 * KAPPA + 30
+                load[e] += 512 * KAPPA + 50
                 hs.append(e)
-            if hs[0] == hs[1]:
-                gather(fn, hs[0], 0, 2)
+            if fn == LAST and hs[0] != hs[1]:
+                for z in (0, 2):
+                    gather(fn, hs[0], z, z + 2)
+                    gather(fn, hs[1], 4 + z, 6 + z)
+            elif hs[0] == hs[1]:
+                gather(fn, hs[0], 0, 8)
             else:
-                gather(fn, hs[0], 0, 1)
-                gather(fn, hs[1], 1, 2)
+                gather(fn, hs[0], 0, 4)
+                gather(fn, hs[1], 4, 8)
             continue
         if E in load and key >= -0.3:
             load[E] += cost
         if fn is not None:
             fn()
     g.wait_ge(T.sem.out, nout[0])
-    g.wait_ge(T.sem.ps, ne)
+    g.wait_ge(T.sem.ps, nps[0])
     g.wait_ge(T.sem.xs, nx)
     g.wait_ge(T.sem.sent, nsent[0])
     for E in ("V", "S", "P", "G"):

from concourse.bass import DstId, RemoteDMATransfer
from concourse.mybir import AluOpType as Op, ActivationFunctionType as Act

MAGIC = 12582912.0
HALF = 2047.5 / 4096.0
CH = 4096
KAPPA = 1.6
FIRST = 3
OWN_CHUNKS = (((0,), (-9, -9, -8.998, -8.997)), ((1,), (-8.9, -8.9, -8.898, -8.897)), ((2, 3), (-8.8, 0.2, 1.2, 1.6)))
FIRST_CHUNKS = (((0, 1), (1.3, 1.8, 2.6, 2.7)), ((2, 3), (1.31, 2.3, 3.6, 4.1)))
LATER_CHUNKS = (-8.2, -6.8, -5.9, -4.7)
BLOCKS = ((0, 1), (2, 3))
GROUPS = ((0, 1), (2,), (3,))
EVAC, EVAC3 = 2.7, 1.6
CREDIT = 3000.0

SCRATCH = {
    "wo": ("sbuf", [128, CH], "bfloat16"), "ws": ("sbuf", [128, CH], "bfloat16"),
    "raw": ("sbuf", [128, 4], "int32"), "pf": ("sbuf", [128, 4], "float32"), "ones": ("sbuf", [128, 4], "float32"),
    "hq": ("sbuf", [128, 1], "int32"), "lr": ("sbuf", [128, 1], "int32"),
    "a0": ("sbuf", [128, 1], "float32"), "a1": ("sbuf", [128, 1], "float32"),
    "mi": ("sbuf", [128, 4], "int32"), "x17": ("sbuf", [128, 1], "int32"), "x48": ("sbuf", [128, 1], "int32"),
    "x49": ("sbuf", [128, 1], "int32"), "m0": ("sbuf", [128, 1], "float32"), "m1": ("sbuf", [128, 1], "float32"),
    "selr": ("sbuf", [128, 1], "float32"), "selq": ("sbuf", [128, 1], "float32"), "one1": ("sbuf", [128, 1], "float32"),
    "sa": ("sbuf", [128, 1], "float32"), "sb": ("sbuf", [128, 1], "float32"), "sc": ("sbuf", [128, 1], "float32"),
    "ic": ("sbuf", [128, 32], "int32"), "cm": ("sbuf", [128, 32], "float32"),
    "itr": ("sbuf", [128, 32], "float32"), "itk": ("sbuf", [128, 32], "float32"), "itm": ("sbuf", [128, 32], "float32"),
    "ie": ("sbuf", [128, 4], "int32"), "iee": ("sbuf", [128, 4], "int32"), "ie2": ("sbuf", [128, 4], "int32"),
    "io1": ("sbuf", [128, 4], "int32"), "oa": ("sbuf", [128, 4], "float32"), "ob": ("sbuf", [128, 4], "float32"),
    "ea": ("sbuf", [128, 4], "float32"), "eb": ("sbuf", [128, 4], "float32"), "e2": ("sbuf", [128, 4], "float16"),
    "jf": ("sbuf", [128, 128], "int32"), "f": ("sbuf", [128, 128], "float32"),
    "fc": ("sbuf", [128, 64], "float32"), "fn": ("sbuf", [128, 64], "float32"),
    "rha": ("sbuf", [128, 512], "float16"), "rhb": ("sbuf", [128, 512], "float16"),
    "l0": ("sbuf", [128, 128], "float16"), "lin": ("sbuf", [128, 512], "float16"),
    "mg": ("sbuf", [128, 512], "bfloat16"), "zer": ("sbuf", [128, 256], "bfloat16"),
    "isel": ("sbuf", [128, 32], "int32"), "sel1": ("sbuf", [128, 32], "bfloat16"), "sel2": ("sbuf", [128, 32], "bfloat16"),
    "isel2": ("sbuf", [128, 16], "int32"), "selb": ("sbuf", [128, 16], "bfloat16"), "onesb": ("sbuf", [128, 128], "bfloat16"),
    "gall": ("sbuf", [128, 32768], "bfloat16"),
    "acc": ("sbuf", [128, 512], "float32"), "tot": ("sbuf", [128, 512], "int32"),
    "ta": ("sbuf", [128, 512], "int32"), "tb": ("sbuf", [128, 512], "int32"),
    "ca": ("sbuf", [128, 512], "bfloat16"), "cb": ("sbuf", [128, 512], "bfloat16"),
    "ysb": ("sbuf", [128, 128], "float32"),
}
for _n in ("A0", "A1", "B0", "B1", "s0", "s1", "xb", "yp"):
    SCRATCH[_n] = ("psum", [128, 512], "float32")
for _d in range(4):
    for _n, _t in (("w", "float32"), ("z", "float32"), ("v", "float32"), ("off", "uint16")):
        SCRATCH["%s%d" % (_n, _d)] = ("sbuf", [128, 512], _t)
    SCRATCH["as%d" % _d] = ("sbuf", [128, 4], "float32")
    if _d:
        SCRATCH["snd%d" % _d] = ("sbuf", [128, 512], "uint16")
        SCRATCH["rcv%d" % _d] = ("sbuf", [128, 512], "uint16")
SEMAPHORES = ["V", "S", "P", "G", "par", "xl", "xs", "xr", "ps", "out", "sent"] + ["pr%d" % k for k in range(4)] \
    + ["ar%d%d" % (d, b) for d in range(1, 4) for b in range(len(BLOCKS))]


def rank_program(g, core, T, topo):
    me = T.rank_of(core)
    if me is None:
        return
    cores = list(T.cores)
    chips = []
    for c in cores:
        if topo.chip(c) not in chips:
            chips.append(topo.chip(c))
    on = [[c for c in cores if topo.chip(c) == ch] for ch in chips]
    k = chips.index(topo.chip(core))
    pos = on[k].index(core)
    sib = [c for c in on[k] if c != core][0]
    q0, q1 = me, T.rank_of(sib)
    peer = [on[(k + d) % 4][pos] for d in range(4)]

    V, S, P = g.vector, g.scalar, g.tensor
    queue = {"V": V, "S": S, "P": P, "G": g, "Y": g.sync}
    cnt = {"V": 0, "S": 0, "P": 0, "G": 0}
    seen = {}

    def em(E, ins):
        ins.then_inc(T.sem[E], 1)
        cnt[E] += 1
        return (E, cnt[E])

    def need(E, *toks):
        best = {}
        for tk in toks:
            if tk is not None:
                best[tk[0]] = max(best.get(tk[0], 0), tk[1])
        for s in best:
            if seen.get((E, s), 0) < best[s]:
                queue[E].wait_ge(T.sem[s], best[s])
                seen[(E, s)] = best[s]

    def gcomp(fn, *a, **kw):
        need("G", ("G", cnt["G"]))
        return em("G", fn(*a, **kw))

    def vs(needs, out, in0, s1, s2, op0, op1=None):
        need("V", *needs)
        if op1 is None:
            return em("V", V.tensor_scalar(out, in0, s1, None, op0))
        return em("V", V.tensor_scalar(out, in0, s1, s2, op0, op1))

    def vt(needs, out, in0, in1, op):
        need("V", *needs)
        return em("V", V.tensor_tensor(out, in0, in1, op))

    for lo, q in ((64, g.sync), (80, S), (96, g.sync), (112, S)):
        q.dma_start(T.raw[lo:lo + 16, 0:1], T.pa[:, :]).then_inc(T.sem.par, 16)
        if lo == 64:
            q.dma_start(T.raw[0:64, 0:4], T.de[:, :]).then_inc(T.sem.par, 16)
    for c in range(4):
        for hh, q in ((0, g.sync), (1, S)):
            q.dma_start(T.wo[32 * c + 16 * hh:32 * c + 16 * hh + 16, :], T.x[:, CH * c:CH * c + CH]).then_inc(T.sem.xl, 16)

    imp = {"allow_small_or_imprecise_dtypes": True}
    i1 = gcomp(g.iota, T.mi[64:128, :], [[0, 4]], 0, 1)
    gcomp(g.iota, T.itr[64:96, :], [[0, 8], [1, 4]], -1, 0, **imp)
    i6 = gcomp(g.iota, T.itk[64:96, :], [[0, 2], [4, 4], [0, 4]], -8, 0, **imp)
    gcomp(g.iota, T.ic[0:64, :], [[8, 2], [0, 16]], 0, 1)
    i7 = gcomp(g.iota, T.ic[64:128, :], [[8, 2], [0, 16]], 0, 4)
    gcomp(g.iota, T.ie[0:64, :], [[-16, 4]], 0, 1)
    i2 = gcomp(g.iota, T.ie[64:128, :], [[-4, 4]], 0, 1)
    gcomp(g.iota, T.fc[96:128, :], [[16, 8], [128, 8]], 9, 0, **imp)
    i4 = gcomp(g.iota, T.fn[96:128, :], [[0, 8], [1, 8]], 0, 0, **imp)
    i5 = gcomp(g.iota, T.jf[0:64, :], [[q0 - q1, 2], [0, 64]], -q0, 1)

    hi = slice(64, 128)
    ands = Op.bitwise_and
    o1 = em("V", V.memset(T.ones[:, :], 1.0))
    vs([i1], T.x17[hi, :], T.mi[hi, 0:1], 17, None, ands)
    vs([], T.x49[hi, :], T.mi[hi, 0:1], 49, None, ands)
    xc = vs([], T.x48[hi, :], T.mi[hi, 0:1], 48, None, ands)
    vs([xc], T.m0[hi, :], T.x17[hi, :], 0, None, Op.is_equal)
    vs([], T.m1[hi, :], T.x17[hi, :], 16, None, Op.is_equal)
    b3 = vs([], T.one1[hi, :], T.x49[hi, :], 1, None, Op.is_equal)
    vs([], T.selr[hi, :], T.x48[hi, :], 48, None, Op.is_equal)
    b4 = vs([], T.sa[hi, :], T.x49[hi, :], 49, 128.0, Op.is_equal, Op.mult)
    need("S", b3, i6)
    em("S", S.activation(T.itr[64:96, :], T.itr[64:96, :], Act.Copy, scale=T.m0[64:96, :]))
    h1 = em("S", S.activation(T.itk[64:96, :], T.itk[64:96, :], Act.Identity, bias=T.one1[64:96, :], scale=T.m1[64:96, :]))
    need("S", i4)
    em("S", S.activation(T.fc[96:128, :], T.fc[96:128, :], Act.Copy, scale=T.m0[96:128, :]))
    g2 = em("S", S.activation(T.fn[96:128, :], T.fn[96:128, :], Act.Copy, scale=T.m1[96:128, :]))
    c1 = vs([b4], T.sb[hi, :], T.selr[hi, :], -1.0, T.sa[hi, :], Op.mult, Op.add)
    h2 = vs([i7], T.ic[:, :], T.ic[:, :], 8, None, ands)
    c3 = vs([c1], T.sc[hi, :], T.one1[hi, :], -1.0, T.sb[hi, :], Op.mult, Op.add)
    h4 = vs([h2], T.cm[:, :], T.ic[:, :], 0, None, Op.is_equal)
    h3 = vt([h1], T.itm[64:96, :], T.itr[64:96, :], T.itk[64:96, :], Op.add)
    c4 = vs([c3], T.selq[hi, :], T.sc[hi, :], 1.0, None, Op.add)
    h5 = vt([h3, h4], T.cm[64:96, :], T.cm[64:96, :], T.itm[64:96, :], Op.mult)
    vs([i2], T.iee[0:64, :], T.ie[0:64, :], 48, None, ands)
    vs([], T.iee[hi, :], T.ie[hi, :], 13, None, ands)
    vs([], T.io1[64:96, :], T.ie[64:96, :], 61, None, ands)
    xf = vs([], T.ie2[96:128, :], T.ie[96:128, :], -3, None, ands)

    V.wait_ge(T.sem.par, 80)
    vs([], T.hq[hi, :], T.raw[hi, 0:1], 7, None, Op.arith_shift_right)
    p1 = vs([], T.lr[hi, :], T.raw[hi, 0:1], 127, None, ands)
    vs([], T.pf[0:64, :], T.raw[0:64, :], 2048.0, None, Op.subtract)
    p2 = vs([p1, c4], T.a0[hi, :], T.hq[hi, :], T.selq[hi, :], T.one1[hi, :], Op.mult, Op.add)
    p3 = vs([p2], T.a1[hi, :], T.lr[hi, :], T.selr[hi, :], T.a0[hi, :], Op.mult, Op.add)
    p4 = vs([p3, o1], T.pf[hi, :], T.ones[hi, :], T.a1[hi, :], None, Op.mult)
    for c in range(4):
        l0 = vs([p4, h5], T.l0[:, 32 * c:32 * c + 32], T.cm[:, :], T.pf[:, c:c + 1], None, Op.mult)
    need("G", l0)
    nps = [0]
    came = {}
    for ds in ((3,), (2, 1)):
        m = topo.mask(core, peer[ds[0]]) & topo.mask(core, peer[ds[-1]])
        ne = bin(m).count("1")
        nps[0] += ne
        ids, outs = [], []
        for d in ds:
            came[4 - d] = ne
            rid, pid, _se = topo.addr(peer[d])
            ids.append(DstId(rid=rid, pnc=pid))
            outs.append(T.lin[:, 128 * (4 - d):128 * (4 - d) + 128])
        g.remote_dma_fused([RemoteDMATransfer(dst_ids=ids, dma_engine_mask=m, remote_sem=T.sem["pr%d" % k],
                                              srcs=[T.l0[:, :]], dsts=outs)], local_sem=T.sem.ps)
    a8 = gcomp(g.iota, T.isel[:, :], [[-1, 32]], 0, 1)

    b5 = vs([xf], T.ea[:, :], T.iee[:, :], 0, 1.0 / 2048, Op.is_equal, Op.mult)
    vs([], T.oa[64:96, :], T.io1[64:96, :], 1, -1023.5 / 2048, Op.is_equal, Op.mult)
    vs([], T.ob[64:96, :], T.io1[64:96, :], 1, -127.5 / 256, Op.is_equal, Op.mult)
    f0 = vs([i5], T.jf[0:64, :], T.jf[0:64, :], 7, None, ands)
    c2 = vs([b5], T.eb[:, :], T.ea[:, :], 8.0, None, Op.mult)
    vt([g2], T.f[96:128, 0:64], T.fc[96:128, :], T.fn[96:128, :], Op.add)
    f2 = vt([], T.f[96:128, 64:128], T.fc[96:128, :], T.fn[96:128, :], Op.add)
    vt([c2], T.ea[64:96, :], T.ea[64:96, :], T.oa[64:96, :], Op.add)
    d2 = vt([], T.eb[64:96, :], T.eb[64:96, :], T.ob[64:96, :], Op.add)
    em("V", V.memset(T.f[64:96, :], 1.0))
    f1 = vs([f0], T.f[0:64, :], T.jf[0:64, :], 0, 256.0, Op.is_equal, Op.mult)
    rh = {}

    def right(p):
        vs([f1, f2, d2], T.rha[:, 128 * p:128 * p + 128], T.f[:, :], T.ea[:, p:p + 1], None, Op.mult)
        rh[p] = vs([], T.rhb[:, 128 * p:128 * p + 128], T.f[:, :], T.eb[:, p:p + 1], None, Op.mult)

    em("V", V.memset(T.mg[0:1, :], MAGIC))
    ob = em("V", V.memset(T.onesb[0:1, :], 1.0))
    right(0)
    e2 = vs([], T.e2[96:128, :], T.ie2[96:128, :], 49, 1.0 / 4096, Op.is_equal, Op.mult)

    g.wait_ge(T.sem.xl, 128)
    rid, pid, _se = topo.addr(sib)
    g.remote_dma(T.ws[:, :], T.wo[:, :], T.sem.xr, T.sem.xs, pid, rid, topo.mask(core, sib))
    nx = len(topo.engines(core, sib))

    units = [(0, p, 0) for p in range(FIRST)] + [(1, p, 0) for p in range(4)] + [(1, p, 1) for p in range(4)]
    for d in (2, 3):
        units += [(d, p, w) for p in range(4) for w in (0, 1)]
    units += [(0, p, 0) for p in range(FIRST, 4)] + [(0, p, 1) for p in range(4)]
    at = {u: float(i) for i, u in enumerate(units)}
    END = float(len(units))
    LAST = units[-1]
    items = []
    tok = {}
    gat = {u: [] for u in units}
    use = {n: [] for n in ("A0", "A1", "B0", "B1", "s0", "s1", "xb", "yp")}
    used = [0, 0]
    chunkno, chunkof = {}, {}

    def put(key, E, fn, cost=0.0):
        items.append((key, len(items), E, fn, cost))

    def span(ps):
        return 128 * ps[0], 128 * ps[-1] + 128

    def chunk(d, ps, keys, first):
        i = len(chunkno) % 2
        chunkno[d, ps] = i
        for p in ps:
            chunkof[d, p] = ps
        lo, hi = span(ps)
        n = hi - lo
        an, bn = "A%d" % i, "B%d" % i
        A, B = T[an], T[bn]
        W, Z, VV, OFF, AS = [T["%s%d" % (nm, d)] for nm in ("w", "z", "v", "off", "as")]

        def times():
            if d and first:
                P.wait_ge(T.sem["pr%d" % ((k + d) % 4)], came[d])
            assert len(use[an]) == len(use[bn]) == used[i]
            used[i] += 1
            need("P", l0, rh[ps[-1]], e2, ob, *(use[an] + use[bn]))
            L = T.lin[:, 128 * d:128 * d + 128] if d else T.l0[:, :]
            for bank, r in ((A, T.rha), (B, T.rhb)):
                P.matmul(bank[:, 0:n], L, r[:, lo:hi], True, False)
                tok[bank is A, d, ps] = em("P", P.matmul(bank[:, 0:n], T.onesb[0:1, :], T.mg[0:1, 0:n], False, True))
                if first and bank is A:
                    need("P", *use["yp"])
                    L2 = T.lin[96:128, 128 * d:128 * d + 128] if d else T.l0[96:128, :]
                    tok["ap", d] = em("P", P.matmul(T.yp[:, 4 * d:4 * d + 4], L2, T.e2[96:128, :], True, True))

        def squares():
            need("S", tok[True, d, ps])
            a = em("S", S.activation(W[:, lo:hi], A[:, 0:n], Act.Square, bias=256.0 - MAGIC))
            use[an].append(a)
            if first:
                need("S", tok["ap", d])
                tok["as", d] = em("S", S.activation(AS[:, :], T.yp[:, 4 * d:4 * d + 4], Act.Copy))
                use["yp"].append(tok["as", d])
            need("S", a, tok["as", d])
            for p in ps:
                c = 128 * p
                tok["z", d, ps] = em("S", S.activation(Z[:, c:c + 128], W[:, c:c + 128], Act.Identity, bias=-HALF, scale=AS[:, p:p + 1]))

        def part0():
            need("V", tok["z", d, ps], tok[False, d, ps])
            tok["v", d, ps] = em("V", V.tensor_tensor(VV[:, lo:hi], B[:, 0:n], Z[:, lo:hi], Op.add))
            use[bn].append(tok["v", d, ps])

        def part1():
            tok["off", d, ps] = vs([tok["v", d, ps]], OFF[:, lo:hi], VV[:, lo:hi], MAGIC - 2048, None, Op.subtract)

        put(keys[0], "P", times)
        put(keys[1], "S", squares, 2 * n + 64 * first)
        put(keys[2], "V", part0, n)
        put(keys[3], "V", part1, n)

    def ucol(u):
        return 1024 * units.index(u)

    def gather(u, E, z0, z1):
        d, p, w = u
        need_x = ("xr", nx) if w else ("xl", 128)
        if (need_x, E) not in tok:
            tok[need_x, E] = 1
            queue[E].wait_ge(T.sem[need_x[0]], need_x[1])
        need(E, tok["off", d, chunkof[d, p]])
        o = 128 * p + 64 * w
        c = ucol(u)
        ind = (T.ws if w else T.wo)[:, 0:CH].indirect(T["off%d" % d][:, o + 8 * z0:o + 8 * z1])
        out = T.gall[:, c + 128 * z0:c + 128 * z1]
        gat[u].append((z0, z1, em(E, V.tensor_copy(out, ind) if E == "V" else S.activation(out, ind, Act.Copy))))

    sl = {}
    nsent, nout = [0], [0]
    nb = [0]

    def summing(bank, ps, d, lazy):
        B = T[bank]
        opened = []

        def one(u, z, start, stop):
            c = ucol(u) + 128 * z
            c0 = 128 * (u[1] - ps[0]) + 32 * (z % 4)
            return P.matmul(B[:, c0:c0 + 32], T.gall[:, c:c + 128], (T.sel2 if z > 3 else T.sel1)[:, :], start, stop)

        def whole(p):
            def fn():
                need("P", sl[0], *([t for w in (0, 1) for _a, _b, t in gat[d, p, w]] + use[bank]))
                for z in range(4):
                    for i, (w, zz) in enumerate(((0, z), (0, z + 4), (1, z), (1, z + 4))):
                        ins = one((d, p, w), zz, i == 0, i == 3)
                tok["sum", d, p] = em("P", ins)
            return fn

        def part(p, w, last):
            def fn():
                if not opened:
                    opened.append(1)
                    n = 128 * len(ps)
                    need("P", ob, tok["zer"], *use[bank])
                    P.matmul(B[:, 0:n], T.onesb[0:1, :], T.zer[0:1, 0:n], True, False)
                need("P", sl[0])
                todo = sorted(gat[d, p, w], key=lambda q: (q[0] % 4, q[0]))
                for i, (z0, z1, t) in enumerate(todo):
                    need("P", t)
                    for z in range(z0, z1):
                        ins = one((d, p, w), z, False, last and i == len(todo) - 1 and z == z1 - 1)
                tok["sum", d, p] = em("P", ins)
            return fn

        for p in ps:
            if not lazy:
                put(at[d, p, 1] + 0.5, "P", whole(p))
            else:
                for w in (0, 1):
                    put(max(at[d, p, w] + (0.5 if d else 0.4), 21.5 + .01 * p), "P", part(p, w, w == 1 and p == ps[-1]))

    def block(d, j, ps):
        bank = "s%d" % (nb[0] % 2)
        nb[0] += 1
        lo, hi = span(ps)
        summing(bank, ps, d, d == 3 and j == len(BLOCKS) - 1)

        def evac():
            need("V", *[tok["sum", d, p] for p in ps])
            tok["ev", d, j] = em("V", V.tensor_copy(T["snd%d" % d][:, lo:hi], T[bank][:, 0:hi - lo]))
            use[bank].append(tok["ev", d, j])

        def send():
            need("G", tok["ev", d, j])
            rid, pid, _se = topo.addr(peer[d])
            g.remote_dma(T["rcv%d" % d][:, lo:hi], T["snd%d" % d][:, lo:hi], T.sem["ar%d%d" % (d, j)], T.sem.sent,
                         pid, rid, topo.mask(core, peer[d]))
            nsent[0] += len(topo.engines(core, peer[d]))

        key = at[d, ps[-1], 1] + (EVAC3 if d == 3 else EVAC)
        put(key, "V", evac, 128 * len(ps))
        put(key, "G", send)

    def unpack(d, j, ps):
        lo, hi = span(ps)

        def fn():
            V.wait_ge(T.sem["ar%d%d" % (d, j)], len(topo.engines(peer[4 - d], core)))
            R = T["rcv%d" % d]
            if d == 1:
                t = em("V", V.tensor_copy(T.acc[:, lo:hi], R[:, lo:hi]))
            else:
                need("V", *use["xb"])
                a = em("V", V.tensor_copy(T.xb[:, lo:hi], R[:, lo:hi]))
                need("V", a, *[tok["acc", p] for p in ps])
                t = em("V", V.tensor_tensor(T.acc[:, lo:hi], T.acc[:, lo:hi], T.xb[:, lo:hi], Op.add))
                use["xb"].append(t)
            for p in ps:
                tok["acc", p] = t
        return fn

    def finish(j, ps, bank):
        lo, hi = span(ps)

        def fn():
            t = vt([tok["acc", p] for p in ps] + [tok["sum", 0, p] for p in ps],
                   T.tot[:, lo:hi], T.acc[:, lo:hi], T[bank][:, 0:hi - lo], Op.add)
            use[bank].append(t)
            x1 = vs([t], T.ta[:, lo:hi], T.tot[:, lo:hi], 511, None, Op.bitwise_and)
            x2 = vs([], T.tb[:, lo:hi], T.tot[:, lo:hi], 9, None, Op.arith_shift_right)
            tok["ca", j] = vs([x1], T.ca[:, lo:hi], T.ta[:, lo:hi], 255, None, Op.min)
            tok["cb", j] = vs([x2], T.cb[:, lo:hi], T.tb[:, lo:hi], 255, None, Op.min)
        return fn

    def turn(j, ps, bank):
        def fn():
            need("P", sl[0], tok["ca", j], *use[bank])
            for z in range(8):
                if z == 4:
                    need("P", tok["cb", j])
                for p in ps:
                    c = 128 * p + 32 * (z % 4)
                    ins = P.matmul(T[bank][32 * p:32 * p + 32, 16 * z:16 * z + 16], (T.cb if z > 3 else T.ca)[:, c:c + 32],
                                   T.selb[:, :], True, True)
            tok["turn", j] = em("P", ins)
        return fn

    def leave(j, ps, bank):
        lo, hi = 32 * ps[0], 32 * ps[-1] + 32

        def fn():
            need("S", tok["turn", j])
            t = em("S", S.activation(T.ysb[lo:hi, :], T[bank][lo:hi, 0:128], Act.Copy))
            need("Y", t)
            g.sync.dma_start(T.y[lo:hi, :], T.ysb[lo:hi, :]).then_inc(T.sem.out, 16)
            nout[0] += 16
        return fn

    def later():
        right(2)
        right(3)
        tok["zer"] = em("V", V.memset(T.zer[0:1, :], 0.0))

    def selections():
        x = vs([a8], T.isel[:, :], T.isel[:, :], 31, None, Op.bitwise_and)
        y = vs([x], T.isel2[:, :], T.isel[:, 0:16], 15, None, Op.bitwise_and)
        vs([y], T.selb[:, :], T.isel2[:, :], 0, None, Op.is_equal)
        vs([], T.sel1[:, :], T.isel[:, :], 0, None, Op.is_equal)
        sl[0] = vs([], T.sel2[:, :], T.isel[:, :], 0, 512.0, Op.is_equal, Op.mult)

    put(-9.5, "V", lambda: right(1))
    put(-8.85, "V", later)
    for i, (ps, keys) in enumerate(OWN_CHUNKS):
        chunk(0, ps, keys, i == 0)
    put(3.5, "V", selections, 320)
    for i, (ps, keys) in enumerate(FIRST_CHUNKS):
        chunk(1, ps, keys, i == 0)
    for d in (2, 3):
        for i, ps in enumerate(BLOCKS):
            chunk(d, ps, [at[d, ps[0], 0] + c for c in LATER_CHUNKS], i == 0)
    for d in (1, 2, 3):
        for j, ps in enumerate(BLOCKS):
            block(d, j, ps)
            key = END + 0.01 + 0.09 * j if d == 3 else min(at[d, ps[-1], 1] + 9.2, END - 0.09)
            put(key, "V", unpack(d, j, ps), 256 * len(ps))
    for j, ps in enumerate(GROUPS):
        bank, out = ("A0", "A1", "B0")[j], ("yp", "B1", "s0")[j]
        summing(bank, ps, 0, True)
        key = END + 0.05 * (1, 3, 4)[j]
        put(key, "V", finish(j, ps, bank))
        put(key + 0.02, "P", turn(j, ps, out))
        put(key + 0.9, "S", leave(j, ps, out))
    put(END - 5.01, "V", None, CREDIT)
    for u in units:
        put(at[u], "GATHER", u)

    items.sort(key=lambda it: (it[0], it[1]))
    load = {"V": 0.0, "S": 0.0}
    for key, _i, E, fn, cost in items:
        if E == "GATHER":
            hs = []
            for h in (0, 1):
                e = "V" if load["V"] <= load["S"] else "S"
                load[e] += 512 * KAPPA + 50
                hs.append(e)
            if fn == LAST and hs[0] != hs[1]:
                for z in (0, 2):
                    gather(fn, hs[0], z, z + 2)
                    gather(fn, hs[1], 4 + z, 6 + z)
            elif hs[0] == hs[1]:
                gather(fn, hs[0], 0, 8)
            else:
                gather(fn, hs[0], 0, 4)
                gather(fn, hs[1], 4, 8)
            continue
        if E in load and key >= -0.3:
            load[E] += cost
        if fn is not None:
            fn()
    g.wait_ge(T.sem.out, nout[0])
    g.wait_ge(T.sem.ps, nps[0])
    g.wait_ge(T.sem.xs, nx)
    g.wait_ge(T.sem.sent, nsent[0])
    for E in ("V", "S", "P", "G"):
        need("G", (E, cnt[E]))
